import numpy as np
import ml_dtypes


def mxq(x, axis, fmt="e4m3"):
    dtype, down = {"e4m3": (ml_dtypes.float8_e4m3fn, 7), "e5m2": (ml_dtypes.float8_e5m2, 14)}[fmt]
    v = np.moveaxis(np.asarray(x, np.float32).astype(ml_dtypes.bfloat16).astype(np.float64), axis, -1)
    blocks = v.reshape(v.shape[:-1] + (-1, 32))
    amax = np.abs(blocks).max(-1, keepdims=True)
    byte = np.maximum(np.where(amax > 0, np.frexp(amax)[1] - 1 + 127, 0) - down, 1)
    scale = np.exp2(byte - 127.0)
    codes = (blocks / scale).astype(np.float32).astype(dtype).astype(np.float64)
    return np.moveaxis((codes * scale).reshape(v.shape), -1, axis)


WIDE = False


def mx_kscale(k):
    if not WIDE:
        return np.ones(k)
    levels = np.array([10, -10, 5, -5, 0])
    if k % 512:
        return np.exp2(np.random.permutation(np.resize(levels, k // 32))).repeat(32)
    a = np.empty((k // 512, 16))
    for p in range(k // 512):
        a[p, :8] = np.random.permutation(np.resize(levels, 8))
        for g in range(8):
            far = levels[np.abs(levels - a[p, g]) >= 10]
            a[p, g + 8] = far[np.random.randint(len(far))]
    return np.exp2(a.ravel()).repeat(32)


def f64(x):
    return np.asarray(x).astype(np.float64)


def striped(idx):
    return np.tile(idx.reshape(-1, 16).T, (8, 1)).astype(np.uint16)


def unstriped(offs):
    return offs[:16].T.reshape(-1).astype(np.int64)


def striped8(idx):
    return np.concatenate([x.reshape(-1, 16).T for x in idx]).astype(np.uint16)


def runs(offs, k):
    lists = np.stack([offs[16 * r : 16 * r + 16].T.reshape(-1) for r in range(8)]).astype(np.int64)
    return lists[np.arange(k) % 512 // 64]


def pack_weight(w):
    k, n = w.shape
    w = f64(np.asarray(w, np.float32).astype(ml_dtypes.bfloat16)).reshape(k // 32, 32, n)
    amax = np.abs(w).max(1)
    byte = np.clip(np.where(amax > 0, np.frexp(amax)[1] - 1 + 127 - 7, 1), 1, 254)
    scaled = (w * np.exp2(127.0 - byte)[:, None, :]).reshape(k, n).astype(np.float32)
    words = np.ascontiguousarray(scaled.reshape(k // 512, 128, 4, n).transpose(0, 1, 3, 2)).astype(ml_dtypes.float8_e4m3fn).view(np.uint8)
    return words, np.ascontiguousarray(byte.astype(np.uint8).reshape(k // 512, 16, n))


def unpack_weight(words, scales):
    g, p, n, _ = words.shape
    vals = np.ascontiguousarray(words).view(ml_dtypes.float8_e4m3fn).astype(np.float64) * np.repeat(np.exp2(scales.astype(np.float64) - 127.0), 8, axis=1)[..., None]
    return vals.transpose(0, 1, 3, 2).reshape(g * 512, n)


E2M1 = np.array([0.0, 0.5, 1.0, 1.5, 2.0, 3.0, 4.0, 6.0, -0.0, -0.5, -1.0, -1.5, -2.0, -3.0, -4.0, -6.0])


def pack_fp4(w):
    k, n = w.shape
    w = f64(np.asarray(w, np.float32).astype(ml_dtypes.bfloat16)).reshape(k // 32, 32, n)
    amax = np.abs(w).max(1)
    mant, ex = np.frexp(amax / 6.0)
    byte = np.clip(np.where(amax > 0, np.where(mant > 0.5, ex, ex - 1) + 127, 1), 1, 254)
    scaled = (w * np.exp2(127.0 - byte)[:, None, :]).reshape(k, n).astype(np.float32)
    c = np.ascontiguousarray(scaled.reshape(k // 512, 128, 4, n).transpose(0, 1, 3, 2)).astype(ml_dtypes.float4_e2m1fn).view(np.uint8) & 0xF
    words = (c[..., 0::2] | (c[..., 1::2] << 4)).reshape(k // 512, 128, 2 * n)
    return np.ascontiguousarray(words), np.ascontiguousarray(byte.astype(np.uint8).reshape(k // 512, 16, n))


def unpack_fp4(words, scales):
    g, _, n = scales.shape
    words = np.ascontiguousarray(words).reshape(g, 128, n, 2)
    nib = np.empty((g, 128, n, 4), np.uint8)
    nib[..., 0::2] = words & 0xF
    nib[..., 1::2] = words >> 4
    vals = E2M1[nib] * np.repeat(np.exp2(scales.astype(np.float64) - 127.0), 8, axis=1)[..., None]
    return vals.transpose(0, 1, 3, 2).reshape(g * 512, n)


def relu(v):
    return np.maximum(v, 0.0)

def planes(y):
    n, m = y.shape
    v = y.astype(np.float32).astype(ml_dtypes.bfloat16).astype(np.float64).reshape(n // 32, 32, m)
    top = np.abs(v).max(1)
    byte = np.clip(np.where(top > 0, np.frexp(top)[1] - 1 + 127 - 7, 1), 1, 254)
    codes = (v * np.exp2(127.0 - byte)[:, None, :]).reshape(n, m).astype(np.float32).astype(ml_dtypes.float8_e4m3fn).view(np.uint8)
    words = codes.reshape(n // 512, 128, 4, m).transpose(0, 1, 3, 2)
    return np.ascontiguousarray(words), np.ascontiguousarray(byte.astype(np.uint8).reshape(n // 512, 16, m))


K, T, S, N, H, U = 512, 2048, 512, 512, 512, 512


def setup_inputs():
    n = np.random.standard_normal
    s = mx_kscale(K)[:, None]
    u = mx_kscale(H)
    packed_xT = pack_weight(n((K, T)) * s)
    packed_w2 = pack_fp4(n((H, N)) / np.sqrt(H) / u[:, None])
    return {
        "x_words": packed_xT[0],
        "x_scales": packed_xT[1],
        "w1": (n((K, H)) / np.sqrt(K) / s * u).astype(np.float32),
        "rin": np.random.uniform(0.5, 1.5, (H, U)).astype(np.float32),
        "w2_words": packed_w2[0],
        "w2_scales": packed_w2[1],
        "so": np.random.uniform(0.5, 1.5, (N, U)).astype(np.float32),
        "offs": striped(np.random.permutation(T)[:S]),
        "mem": striped8(np.stack([np.random.permutation(U)[(U * np.random.uniform(0, 1, S) ** 4).astype(np.int64)] for _ in range(8)])),
    }


def reference(x_words, x_scales, w1, rin, w2_words, w2_scales, so, offs, mem):
    xq = unpack_weight(x_words, x_scales)[:, unstriped(offs)]
    h = relu(mxq(f64(w1), 0, "e4m3").T @ xq)
    z = h * (f64(rin)[np.arange(H)[:, None], runs(mem, H)])
    o = unpack_fp4(w2_words, w2_scales).T @ mxq(z, 0, "e4m3")
    out_0 = o * (f64(so)[np.arange(N)[:, None], runs(mem, N)])
    return (out_0,) + planes(out_0)

@@ -1,0 +1,188 @@
+from contextlib import ExitStack
+
+import concourse.mybir as mybir
+
+F32 = mybir.dt.float32
+BF16 = mybir.dt.bfloat16
+I32 = mybir.dt.int32
+U32 = mybir.dt.uint32
+U16 = mybir.dt.uint16
+U8 = mybir.dt.uint8
+FP8X4 = mybir.dt.float8_e4m3fn_x4
+FP4X4 = mybir.dt.float4_e2m1fn_x4
+RELU = mybir.ActivationFunctionType.Relu
+MULT = mybir.AluOpType.mult
+
+P = 128
+PACK = 4
+T = 2048
+S = 512
+W = 512
+HALF = 256
+CH = 128
+NCH = S // CH
+
+FLOPS = 2 * 2 * 512 * 512 * 512
+
+
+def tile_picked_bens8_relu_po_kernel(
+    tc, x_words, x_scales, w1, rin, w2_words, w2_scales, so, offs, mem, out_0, out_1, out_2
+):
+    nc = tc.nc
+    with ExitStack() as ctx:
+        keep = ctx.enter_context(tc.tile_pool(name="keep", bufs=1))
+        psum = ctx.enter_context(tc.psum_pool(name="psum", bufs=4))
+
+        def tile(name, shape, dtype):
+            return keep.tile(shape, dtype, name=name, align_bytes=64)
+
+        offs_sb = tile("offs_sb", [P, S // 16], U16)
+        mem_sb = tile("mem_sb", [P, S // 16], U16)
+        xw_all = tile("xw_all", [P, T], I32)
+        xs_all = tile("xs_all", [P, T], U8)
+        w1_raw = tile("w1_raw", [P, PACK, W], F32)
+        w2w_raw = tile("w2w_raw", [P, 2 * W], U8)
+        w2s_raw = tile("w2s_raw", [P, W], U8)
+        rin_sb = [tile(f"rin{t}", [P, W], F32) for t in range(PACK)]
+        so_sb = [tile(f"so{t}", [P, W], F32) for t in range(PACK)]
+
+        nc.vector.memset(xs_all[:].bitcast(I32), 0)
+        nc.gpsimd.memset(w2s_raw[:].bitcast(I32), 0)
+
+        nc.sync.dma_start(offs_sb[:], offs)
+        nc.sync.dma_start(w2w_raw[:].bitcast(I32), w2_words[0].bitcast(I32))
+        nc.sync.dma_start(w1_raw[:], w1.rearrange("(p j) c -> p j c", j=PACK))
+        for q in range(4):
+            nc.scalar.dma_start(
+                xs_all[32 * q : 32 * q + 4, :].bitcast(I32), x_scales[0, 4 * q : 4 * q + 4, :].bitcast(I32)
+            )
+        nc.sync.dma_start(xw_all[:], x_words[0].rearrange("p c r -> p (c r)").bitcast(I32))
+        for q in range(4):
+            nc.gpsimd.dma_start(
+                w2s_raw[32 * q : 32 * q + 4, :].bitcast(I32), w2_scales[0, 4 * q : 4 * q + 4, :].bitcast(I32)
+            )
+        nc.sync.dma_start(mem_sb[:], mem)
+        rin_v = rin.rearrange("(p t) u -> t p u", t=PACK)
+        so_v = so.rearrange("(p t) u -> t p u", t=PACK)
+        for t in range(PACK):
+            nc.sync.dma_start(rin_sb[t][:], rin_v[t])
+        for t in range(PACK):
+            nc.sync.dma_start(so_sb[t][:], so_v[t])
+
+        w2w = tile("w2w", [P, 2 * W], U8)
+        w2s = tile("w2s", [P, W], U8)
+        nc.vector.tensor_copy(
+            w2w[:].rearrange("p (t m b) -> p t m b", t=PACK, b=2),
+            w2w_raw[:].rearrange("p (m t b) -> p t m b", t=PACK, b=2),
+        )
+        xs = tile("xs", [P, S], U8)
+        nc.vector.tensor_copy(xs[:], xs_all[:].indirect(offs_sb[:]))
+
+        w1_bf = tile("w1_bf", [P, PACK * W], BF16)
+        w1_dst = w1_bf[:].rearrange("p (t m j) -> p m t j", t=PACK, j=PACK)
+        w1_src = w1_raw[:].rearrange("p j (m t) -> p m t j", t=PACK)
+        split = 88
+        nc.scalar.copy(w1_dst[:, split:], w1_src[:, split:])
+        nc.vector.tensor_copy(w1_dst[:, :split], w1_src[:, :split])
+        nc.vector.tensor_copy(
+            w2s[:].rearrange("p (t m) -> p t m", t=PACK), w2s_raw[:].rearrange("p (m t) -> p t m", t=PACK)
+        )
+        w1w = tile("w1w", [P, W], I32)
+        w1s = tile("w1s", [P, W], U8)
+        nc.vector.quantize_mx(out=w1w[:].bitcast(FP8X4), scales=w1s[:], in_=w1_bf[:])
+
+        xw = [tile(f"xw{h}", [P, HALF], I32) for h in range(2)]
+        hid = [[tile(f"hid{h}_{t}", [P, HALF], F32) for t in range(PACK)] for h in range(2)]
+        for h in range(2):
+            nc.vector.tensor_copy(
+                xw[h][:].bitcast(U32), xw_all[:].bitcast(U32).indirect(offs_sb[:, 16 * h : 16 * h + 16])
+            )
+        for h in range(2):
+            for t in range(PACK):
+                acc = psum.tile([P, HALF], F32, name="acc1")
+                nc.tensor.matmul_mx(
+                    out=acc[:],
+                    lhsT=w1w[:, P * t : P * t + P].bitcast(FP8X4),
+                    lhsT_scale=w1s[:, P * t : P * t + P],
+                    rhs=xw[h][:].bitcast(FP8X4),
+                    rhs_scale=xs[:, HALF * h : HALF * h + HALF],
+                    start=True,
+                    stop=True,
+                )
+                nc.scalar.activation(hid[h][t][:], acc[:], RELU)
+
+        z32 = [tile(f"z32_{c}", [P, PACK, CH], F32) for c in range(NCH)]
+        zbf = [tile(f"zbf_{c}", [P, PACK * CH], BF16) for c in range(NCH)]
+        zw = [tile(f"zw_{c}", [P, CH], I32) for c in range(NCH)]
+        zs = [tile(f"zs_{c}", [P, CH], U8) for c in range(NCH)]
+        o32 = [tile(f"o32_{c}", [P, PACK, CH], F32) for c in range(NCH)]
+        y32 = [tile(f"y32_{c}", [P, PACK, CH], F32) for c in range(NCH)]
+        ybf = [tile(f"ybf_{c}", [P, PACK * CH], BF16) for c in range(NCH)]
+        yw = tile("yw", [P, S], I32)
+        ys = tile("ys", [P, S], U8)
+        out0_v = out_0.rearrange("(p t) n -> p t n", t=PACK)
+        out1_v = out_1[0].rearrange("p c r -> p (c r)").bitcast(I32)
+
+        def members(c):
+            return mem_sb[:, 8 * c : 8 * c + 8]
+
+        def weave(copy, dst, src):
+            copy(
+                dst[:].rearrange("p (c i t) -> p c t i", i=4, t=PACK),
+                src[:].rearrange("p t (c i) -> p c t i", i=4),
+            )
+
+        def scale_hidden(c):
+            h, lo = divmod(c * CH, HALF)
+            for t in range(PACK):
+                nc.vector.tensor_tensor(
+                    z32[c][:, t, :], rin_sb[t][:].indirect(members(c)), hid[h][t][:, lo : lo + CH], MULT
+                )
+            weave(nc.scalar.copy, zbf[c], z32[c])
+
+        def second_product(c):
+            nc.vector.quantize_mx(out=zw[c][:].bitcast(FP8X4), scales=zs[c][:], in_=zbf[c][:])
+            acc = psum.tile([P, PACK, CH], F32, name="acc2")
+            for t in range(PACK):
+                nc.tensor.matmul_mx(
+                    out=acc[:, t, :],
+                    lhsT=w2w[:, 2 * P * t : 2 * P * (t + 1)].bitcast(FP4X4),
+                    lhsT_scale=w2s[:, P * t : P * t + P],
+                    rhs=zw[c][:].bitcast(FP8X4),
+                    rhs_scale=zs[c][:],
+                    start=True,
+                    stop=True,
+                )
+            nc.scalar.copy(o32[c][:], acc[:])
+
+        def scale_output(c):
+            for t in range(PACK):
+                nc.vector.tensor_tensor(y32[c][:, t, :], so_sb[t][:].indirect(members(c)), o32[c][:, t, :], MULT)
+            nc.sync.dma_start(out0_v[:, :, c * CH : (c + 1) * CH], y32[c][:])
+            weave(nc.vector.tensor_copy if c == NCH - 1 else nc.scalar.copy, ybf[c], y32[c])
+
+        def output_planes(c):
+            cols = slice(c * CH, (c + 1) * CH)
+            nc.vector.quantize_mx(out=yw[:, cols].bitcast(FP8X4), scales=ys[:, cols], in_=ybf[c][:])
+
+        scale_hidden(0)
+        scale_hidden(1)
+        second_product(0)
+        scale_hidden(2)
+        second_product(1)
+        scale_output(0)
+        scale_hidden(3)
+        second_product(2)
+        scale_output(1)
+        output_planes(0)
+        second_product(3)
+        scale_output(2)
+        output_planes(1)
+        scale_output(3)
+        output_planes(2)
+        nc.sync.dma_start(out1_v[:, : 3 * CH], yw[:, : 3 * CH])
+        output_planes(3)
+        nc.sync.dma_start(out1_v[:, 3 * CH :], yw[:, 3 * CH :])
+        for q in range(4):
+            eng = nc.scalar if q % 2 else nc.sync
+            eng.dma_start(out_2[0, 4 * q : 4 * q + 4, :].bitcast(I32), ys[32 * q : 32 * q + 4, :].bitcast(I32))

@@ -46,24 +46,24 @@ def tile_picked_bens8_relu_po_kernel(
         rin_sb = [tile(f"rin{t}", [P, W], F32) for t in range(PACK)]
         so_sb = [tile(f"so{t}", [P, W], F32) for t in range(PACK)]
 
-        nc.vector.memset(xs_all[:].bitcast(I32), 0)
+        nc.gpsimd.memset(xs_all[:].bitcast(I32), 0)
         nc.gpsimd.memset(w2s_raw[:].bitcast(I32), 0)
 
         nc.sync.dma_start(offs_sb[:], offs)
         nc.sync.dma_start(w2w_raw[:].bitcast(I32), w2_words[0].bitcast(I32))
         nc.sync.dma_start(w1_raw[:], w1.rearrange("(p j) c -> p j c", j=PACK))
         for q in range(4):
-            nc.scalar.dma_start(
+            nc.sync.dma_start(
                 xs_all[32 * q : 32 * q + 4, :].bitcast(I32), x_scales[0, 4 * q : 4 * q + 4, :].bitcast(I32)
             )
         nc.sync.dma_start(xw_all[:], x_words[0].rearrange("p c r -> p (c r)").bitcast(I32))
-        for q in range(4):
-            nc.gpsimd.dma_start(
-                w2s_raw[32 * q : 32 * q + 4, :].bitcast(I32), w2_scales[0, 4 * q : 4 * q + 4, :].bitcast(I32)
-            )
         nc.sync.dma_start(mem_sb[:], mem)
         rin_v = rin.rearrange("(p t) u -> t p u", t=PACK)
         so_v = so.rearrange("(p t) u -> t p u", t=PACK)
+        for q in range(4):
+            nc.sync.dma_start(
+                w2s_raw[32 * q : 32 * q + 4, :].bitcast(I32), w2_scales[0, 4 * q : 4 * q + 4, :].bitcast(I32)
+            )
         for t in range(PACK):
             nc.sync.dma_start(rin_sb[t][:], rin_v[t])
         for t in range(PACK):
@@ -76,42 +76,45 @@ def tile_picked_bens8_relu_po_kernel(
             w2w_raw[:].rearrange("p (m t b) -> p t m b", t=PACK, b=2),
         )
         xs = tile("xs", [P, S], U8)
-        nc.vector.tensor_copy(xs[:], xs_all[:].indirect(offs_sb[:]))
 
         w1_bf = tile("w1_bf", [P, PACK * W], BF16)
         w1_dst = w1_bf[:].rearrange("p (t m j) -> p m t j", t=PACK, j=PACK)
         w1_src = w1_raw[:].rearrange("p j (m t) -> p m t j", t=PACK)
-        split = 88
+        split = 40
         nc.scalar.copy(w1_dst[:, split:], w1_src[:, split:])
         nc.vector.tensor_copy(w1_dst[:, :split], w1_src[:, :split])
-        nc.vector.tensor_copy(
-            w2s[:].rearrange("p (t m) -> p t m", t=PACK), w2s_raw[:].rearrange("p (m t) -> p t m", t=PACK)
-        )
+        nc.vector.tensor_copy(xs[:], xs_all[:].indirect(offs_sb[:]))
         w1w = tile("w1w", [P, W], I32)
         w1s = tile("w1s", [P, W], U8)
         nc.vector.quantize_mx(out=w1w[:].bitcast(FP8X4), scales=w1s[:], in_=w1_bf[:])
 
         xw = [tile(f"xw{h}", [P, HALF], I32) for h in range(2)]
-        hid = [[tile(f"hid{h}_{t}", [P, HALF], F32) for t in range(PACK)] for h in range(2)]
         for h in range(2):
             nc.vector.tensor_copy(
                 xw[h][:].bitcast(U32), xw_all[:].bitcast(U32).indirect(offs_sb[:, 16 * h : 16 * h + 16])
             )
-        for h in range(2):
-            for t in range(PACK):
-                acc = psum.tile([P, HALF], F32, name="acc1")
-                nc.tensor.matmul_mx(
-                    out=acc[:],
-                    lhsT=w1w[:, P * t : P * t + P].bitcast(FP8X4),
-                    lhsT_scale=w1s[:, P * t : P * t + P],
-                    rhs=xw[h][:].bitcast(FP8X4),
-                    rhs_scale=xs[:, HALF * h : HALF * h + HALF],
-                    start=True,
-                    stop=True,
-                )
-                nc.scalar.activation(hid[h][t][:], acc[:], RELU)
+        nc.vector.tensor_copy(
+            w2s[:].rearrange("p (t m) -> p t m", t=PACK), w2s_raw[:].rearrange("p (m t) -> p t m", t=PACK)
+        )
 
-        z32 = [tile(f"z32_{c}", [P, PACK, CH], F32) for c in range(NCH)]
+        hid = {}
+
+        def first_product(h, t):
+            acc = psum.tile([P, HALF], F32, name="acc1")
+            nc.tensor.matmul_mx(
+                out=acc[:],
+                lhsT=w1w[:, P * t : P * t + P].bitcast(FP8X4),
+                lhsT_scale=w1s[:, P * t : P * t + P],
+                rhs=xw[h][:].bitcast(FP8X4),
+                rhs_scale=xs[:, h * HALF : (h + 1) * HALF],
+                start=True,
+                stop=True,
+            )
+            slot = t if h == 0 else 2 + t % 2
+            hid[h, t] = keep.tile([P, HALF], F32, name=f"hid{h}_{t}", tag=f"hid{slot}", align_bytes=64)
+            nc.scalar.activation(hid[h, t][:], acc[:], RELU)
+
+        z32 = [tile(f"z32_{h}", [P, PACK, HALF], F32) for h in range(2)]
         zbf = [tile(f"zbf_{c}", [P, PACK * CH], BF16) for c in range(NCH)]
         zw = [tile(f"zw_{c}", [P, CH], I32) for c in range(NCH)]
         zs = [tile(f"zs_{c}", [P, CH], U8) for c in range(NCH)]
@@ -129,19 +132,20 @@ def tile_picked_bens8_relu_po_kernel(
         def weave(copy, dst, src):
             copy(
                 dst[:].rearrange("p (c i t) -> p c t i", i=4, t=PACK),
-                src[:].rearrange("p t (c i) -> p c t i", i=4),
+                src.rearrange("p t (c i) -> p c t i", i=4),
             )
 
-        def scale_hidden(c):
+        def scale_hidden(h, t):
+            nc.vector.tensor_tensor(
+                z32[h][:, t, :], rin_sb[t][:].indirect(mem_sb[:, 16 * h : 16 * h + 16]), hid[h, t][:], MULT
+            )
+
+        def round_hidden(c):
             h, lo = divmod(c * CH, HALF)
-            for t in range(PACK):
-                nc.vector.tensor_tensor(
-                    z32[c][:, t, :], rin_sb[t][:].indirect(members(c)), hid[h][t][:, lo : lo + CH], MULT
-                )
-            weave(nc.scalar.copy, zbf[c], z32[c])
+            weave(nc.scalar.copy, zbf[c], z32[h][:, :, lo : lo + CH])
+            nc.vector.quantize_mx(out=zw[c][:].bitcast(FP8X4), scales=zs[c][:], in_=zbf[c][:])
 
         def second_product(c):
-            nc.vector.quantize_mx(out=zw[c][:].bitcast(FP8X4), scales=zs[c][:], in_=zbf[c][:])
             acc = psum.tile([P, PACK, CH], F32, name="acc2")
             for t in range(PACK):
                 nc.tensor.matmul_mx(
@@ -159,26 +163,36 @@ def tile_picked_bens8_relu_po_kernel(
             for t in range(PACK):
                 nc.vector.tensor_tensor(y32[c][:, t, :], so_sb[t][:].indirect(members(c)), o32[c][:, t, :], MULT)
             nc.sync.dma_start(out0_v[:, :, c * CH : (c + 1) * CH], y32[c][:])
-            weave(nc.vector.tensor_copy if c == NCH - 1 else nc.scalar.copy, ybf[c], y32[c])
 
         def output_planes(c):
+            weave(nc.vector.tensor_copy if c == NCH - 1 else nc.scalar.copy, ybf[c], y32[c][:])
             cols = slice(c * CH, (c + 1) * CH)
             nc.vector.quantize_mx(out=yw[:, cols].bitcast(FP8X4), scales=ys[:, cols], in_=ybf[c][:])
 
-        scale_hidden(0)
-        scale_hidden(1)
+        for t in range(PACK):
+            first_product(0, t)
+            scale_hidden(0, t)
+        for t in range(2):
+            first_product(1, t)
+            scale_hidden(1, t)
+        round_hidden(0)
+        first_product(1, 2)
+        scale_hidden(1, 2)
+        round_hidden(1)
+        first_product(1, 3)
+        scale_hidden(1, 3)
         second_product(0)
-        scale_hidden(2)
-        second_product(1)
         scale_output(0)
-        scale_hidden(3)
-        second_product(2)
+        round_hidden(2)
+        second_product(1)
         scale_output(1)
+        round_hidden(3)
+        second_product(2)
+        scale_output(2)
         output_planes(0)
         second_product(3)
-        scale_output(2)
-        output_planes(1)
         scale_output(3)
+        output_planes(1)
         output_planes(2)
         nc.sync.dma_start(out1_v[:, : 3 * CH], yw[:, : 3 * CH])
         output_planes(3)

@@ -12,6 +12,7 @@ FP8X4 = mybir.dt.float8_e4m3fn_x4
 FP4X4 = mybir.dt.float4_e2m1fn_x4
 RELU = mybir.ActivationFunctionType.Relu
 MULT = mybir.AluOpType.mult
+MAX = mybir.AluOpType.max
 
 P = 128
 PACK = 4
@@ -93,9 +94,8 @@ def tile_picked_bens8_relu_po_kernel(
             nc.vector.tensor_copy(
                 xw[h][:].bitcast(U32), xw_all[:].bitcast(U32).indirect(offs_sb[:, 16 * h : 16 * h + 16])
             )
-        nc.vector.tensor_copy(
-            w2s[:].rearrange("p (t m) -> p t m", t=PACK), w2s_raw[:].rearrange("p (m t) -> p t m", t=PACK)
-        )
+        rin_first = tile("rin_first", [P, HALF], F32)
+        nc.vector.tensor_copy(rin_first[:], rin_sb[0][:].indirect(mem_sb[:, :16]))
 
         hid = {}
 
@@ -110,17 +110,27 @@ def tile_picked_bens8_relu_po_kernel(
                 start=True,
                 stop=True,
             )
-            slot = t if h == 0 else 2 + t % 2
-            hid[h, t] = keep.tile([P, HALF], F32, name=f"hid{h}_{t}", tag=f"hid{slot}", align_bytes=64)
-            nc.scalar.activation(hid[h, t][:], acc[:], RELU)
+            if (h, t) == (0, 0):
+                nc.vector.scalar_tensor_tensor(z32[0][:, 0, :], acc[:], 0.0, rin_first[:], MAX, MULT)
+            else:
+                nc.scalar.activation(hid[h, t], acc[:], RELU)
+                nc.vector.tensor_tensor(
+                    z32[h][:, t, :], rin_sb[t][:].indirect(mem_sb[:, 16 * h : 16 * h + 16]), hid[h, t], MULT
+                )
 
         z32 = [tile(f"z32_{h}", [P, PACK, HALF], F32) for h in range(2)]
+        hid_sb = tile("hid_sb", [P, 5, HALF], F32)
+        for t in range(3):
+            hid[0, t] = hid_sb[:, t, :]
+        hid[0, 3] = z32[1][:].rearrange("p t n -> p (t n)")[:, CH : CH + HALF]
+        for t in range(PACK):
+            hid[1, t] = hid_sb[:, 3 + t % 2, :]
         zbf = [tile(f"zbf_{c}", [P, PACK * CH], BF16) for c in range(NCH)]
         zw = [tile(f"zw_{c}", [P, CH], I32) for c in range(NCH)]
         zs = [tile(f"zs_{c}", [P, CH], U8) for c in range(NCH)]
-        o32 = [tile(f"o32_{c}", [P, PACK, CH], F32) for c in range(NCH)]
+        o32 = [z32[0][:, :, :CH], z32[1][:, :, :CH], z32[1][:, :, CH:], z32[0][:, :, CH:]]
         y32 = [tile(f"y32_{c}", [P, PACK, CH], F32) for c in range(NCH)]
-        ybf = [tile(f"ybf_{c}", [P, PACK * CH], BF16) for c in range(NCH)]
+        ybf = [tile(f"ybf_{h}", [P, PACK * HALF], BF16) for h in range(2)]
         yw = tile("yw", [P, S], I32)
         ys = tile("ys", [P, S], U8)
         out0_v = out_0.rearrange("(p t) n -> p t n", t=PACK)
@@ -131,56 +141,57 @@ def tile_picked_bens8_relu_po_kernel(
 
         def weave(copy, dst, src):
             copy(
-                dst[:].rearrange("p (c i t) -> p c t i", i=4, t=PACK),
+                dst.rearrange("p (c i t) -> p c t i", i=4, t=PACK),
                 src.rearrange("p t (c i) -> p c t i", i=4),
-            )
-
-        def scale_hidden(h, t):
-            nc.vector.tensor_tensor(
-                z32[h][:, t, :], rin_sb[t][:].indirect(mem_sb[:, 16 * h : 16 * h + 16]), hid[h, t][:], MULT
             )
 
         def round_hidden(c):
             h, lo = divmod(c * CH, HALF)
-            weave(nc.scalar.copy, zbf[c], z32[h][:, :, lo : lo + CH])
+            weave(nc.scalar.copy, zbf[c][:], z32[h][:, :, lo : lo + CH])
             nc.vector.quantize_mx(out=zw[c][:].bitcast(FP8X4), scales=zs[c][:], in_=zbf[c][:])
 
         def second_product(c):
-            acc = psum.tile([P, PACK, CH], F32, name="acc2")
-            for t in range(PACK):
-                nc.tensor.matmul_mx(
-                    out=acc[:, t, :],
-                    lhsT=w2w[:, 2 * P * t : 2 * P * (t + 1)].bitcast(FP4X4),
-                    lhsT_scale=w2s[:, P * t : P * t + P],
-                    rhs=zw[c][:].bitcast(FP8X4),
-                    rhs_scale=zs[c][:],
-                    start=True,
-                    stop=True,
-                )
-            nc.scalar.copy(o32[c][:], acc[:])
+            step = 2 if c == 0 else PACK
+            for lo in range(0, PACK, step):
+                acc = psum.tile([P, step, CH], F32, name="acc2")
+                for t in range(lo, lo + step):
+                    nc.tensor.matmul_mx(
+                        out=acc[:, t - lo, :],
+                        lhsT=w2w[:, 2 * P * t : 2 * P * (t + 1)].bitcast(FP4X4),
+                        lhsT_scale=w2s[:, P * t : P * t + P],
+                        rhs=zw[c][:].bitcast(FP8X4),
+                        rhs_scale=zs[c][:],
+                        start=True,
+                        stop=True,
+                    )
+                nc.scalar.copy(o32[c][:, lo : lo + step, :], acc[:])
 
         def scale_output(c):
             for t in range(PACK):
                 nc.vector.tensor_tensor(y32[c][:, t, :], so_sb[t][:].indirect(members(c)), o32[c][:, t, :], MULT)
             nc.sync.dma_start(out0_v[:, :, c * CH : (c + 1) * CH], y32[c][:])
 
-        def output_planes(c):
-            weave(nc.vector.tensor_copy if c == NCH - 1 else nc.scalar.copy, ybf[c], y32[c][:])
-            cols = slice(c * CH, (c + 1) * CH)
-            nc.vector.quantize_mx(out=yw[:, cols].bitcast(FP8X4), scales=ys[:, cols], in_=ybf[c][:])
+        def round_output(copy, c, lo, hi):
+            h, base = divmod(c * CH, HALF)
+            weave(copy, ybf[h][:, PACK * (base + lo) : PACK * (base + hi)], y32[c][:, :, lo:hi])
 
-        for t in range(PACK):
+        def output_planes(h):
+            cols = slice(h * HALF, (h + 1) * HALF)
+            nc.vector.quantize_mx(out=yw[:, cols].bitcast(FP8X4), scales=ys[:, cols], in_=ybf[h][:])
+            nc.sync.dma_start(out1_v[:, cols], yw[:, cols])
+
+        first_product(0, 0)
+        nc.vector.tensor_copy(
+            w2s[:].rearrange("p (t m) -> p t m", t=PACK), w2s_raw[:].rearrange("p (m t) -> p t m", t=PACK)
+        )
+        for t in range(1, PACK):
             first_product(0, t)
-            scale_hidden(0, t)
         for t in range(2):
             first_product(1, t)
-            scale_hidden(1, t)
         round_hidden(0)
         first_product(1, 2)
-        scale_hidden(1, 2)
         round_hidden(1)
         first_product(1, 3)
-        scale_hidden(1, 3)
         second_product(0)
         scale_output(0)
         round_hidden(2)
@@ -189,14 +200,15 @@ def tile_picked_bens8_relu_po_kernel(
         round_hidden(3)
         second_product(2)
         scale_output(2)
-        output_planes(0)
+        round_output(nc.scalar.copy, 0, 0, CH)
         second_product(3)
         scale_output(3)
+        round_output(nc.scalar.copy, 1, 0, CH)
+        round_output(nc.scalar.copy, 2, 0, CH)
+        round_output(nc.vector.tensor_copy, 3, 0, 96)
+        round_output(nc.scalar.copy, 3, 96, CH)
+        output_planes(0)
         output_planes(1)
-        output_planes(2)
-        nc.sync.dma_start(out1_v[:, : 3 * CH], yw[:, : 3 * CH])
-        output_planes(3)
-        nc.sync.dma_start(out1_v[:, 3 * CH :], yw[:, 3 * CH :])
         for q in range(4):
             eng = nc.scalar if q % 2 else nc.sync
             eng.dma_start(out_2[0, 4 * q : 4 * q + 4, :].bitcast(I32), ys[32 * q : 32 * q + 4, :].bitcast(I32))

@@ -81,63 +81,53 @@ def tile_picked_bens8_relu_po_kernel(
         w1_bf = tile("w1_bf", [P, PACK * W], BF16)
         w1_dst = w1_bf[:].rearrange("p (t m j) -> p m t j", t=PACK, j=PACK)
         w1_src = w1_raw[:].rearrange("p j (m t) -> p m t j", t=PACK)
+        w1w = [tile(f"w1w{t}", [P, P], I32) for t in range(PACK)]
+        w1s = [tile(f"w1s{t}", [P, P], U8) for t in range(PACK)]
+
+        def quantize_w1(t):
+            nc.vector.quantize_mx(out=w1w[t][:].bitcast(FP8X4), scales=w1s[t][:], in_=w1_bf[:, W * t : W * (t + 1)])
+
         split = 40
         nc.scalar.copy(w1_dst[:, split:], w1_src[:, split:])
         nc.vector.tensor_copy(w1_dst[:, :split], w1_src[:, :split])
         nc.vector.tensor_copy(xs[:], xs_all[:].indirect(offs_sb[:]))
-        w1w = tile("w1w", [P, W], I32)
-        w1s = tile("w1s", [P, W], U8)
-        nc.vector.quantize_mx(out=w1w[:].bitcast(FP8X4), scales=w1s[:], in_=w1_bf[:])
+        for t in range(2):
+            quantize_w1(t)
 
         xw = [tile(f"xw{h}", [P, HALF], I32) for h in range(2)]
-        for h in range(2):
+
+        def pick_words(h):
             nc.vector.tensor_copy(
                 xw[h][:].bitcast(U32), xw_all[:].bitcast(U32).indirect(offs_sb[:, 16 * h : 16 * h + 16])
             )
-        rin_first = tile("rin_first", [P, HALF], F32)
-        nc.vector.tensor_copy(rin_first[:], rin_sb[0][:].indirect(mem_sb[:, :16]))
 
-        hid = {}
-
-        def first_product(h, t):
-            acc = psum.tile([P, HALF], F32, name="acc1")
-            nc.tensor.matmul_mx(
-                out=acc[:],
-                lhsT=w1w[:, P * t : P * t + P].bitcast(FP8X4),
-                lhsT_scale=w1s[:, P * t : P * t + P],
-                rhs=xw[h][:].bitcast(FP8X4),
-                rhs_scale=xs[:, h * HALF : (h + 1) * HALF],
-                start=True,
-                stop=True,
-            )
-            if (h, t) == (0, 0):
-                nc.vector.scalar_tensor_tensor(z32[0][:, 0, :], acc[:], 0.0, rin_first[:], MAX, MULT)
-            else:
-                nc.scalar.activation(hid[h, t], acc[:], RELU)
-                nc.vector.tensor_tensor(
-                    z32[h][:, t, :], rin_sb[t][:].indirect(mem_sb[:, 16 * h : 16 * h + 16]), hid[h, t], MULT
-                )
+        pick_words(0)
+        for t in range(2, PACK):
+            quantize_w1(t)
+        pick_words(1)
+        nc.vector.tensor_copy(
+            w2s[:].rearrange("p (t m) -> p t m", t=PACK), w2s_raw[:].rearrange("p (m t) -> p t m", t=PACK)
+        )
 
         z32 = [tile(f"z32_{h}", [P, PACK, HALF], F32) for h in range(2)]
         hid_sb = tile("hid_sb", [P, 5, HALF], F32)
+        hid = {}
         for t in range(3):
             hid[0, t] = hid_sb[:, t, :]
         hid[0, 3] = z32[1][:].rearrange("p t n -> p (t n)")[:, CH : CH + HALF]
         for t in range(PACK):
             hid[1, t] = hid_sb[:, 3 + t % 2, :]
-        zbf = [tile(f"zbf_{c}", [P, PACK * CH], BF16) for c in range(NCH)]
-        zw = [tile(f"zw_{c}", [P, CH], I32) for c in range(NCH)]
-        zs = [tile(f"zs_{c}", [P, CH], U8) for c in range(NCH)]
-        o32 = [z32[0][:, :, :CH], z32[1][:, :, :CH], z32[1][:, :, CH:], z32[0][:, :, CH:]]
-        y32 = [tile(f"y32_{c}", [P, PACK, CH], F32) for c in range(NCH)]
-        ybf = [tile(f"ybf_{h}", [P, PACK * HALF], BF16) for h in range(2)]
+        spans = [(0, HALF), (HALF, HALF + CH), (HALF + CH, S)]
+        zbf = [tile(f"zbf_{c}", [P, PACK * (hi - lo)], BF16) for c, (lo, hi) in enumerate(spans)]
+        zw = [tile(f"zw_{c}", [P, hi - lo], I32) for c, (lo, hi) in enumerate(spans)]
+        zs = [tile(f"zs_{c}", [P, hi - lo], U8) for c, (lo, hi) in enumerate(spans)]
+        o32 = [tile(f"o32_{c}", [P, PACK, hi - lo], F32) for c, (lo, hi) in enumerate(spans)]
+        y32 = [tile(f"y32_{c}", [P, PACK, hi - lo], F32) for c, (lo, hi) in enumerate(spans)]
+        ybf = [tile(f"ybf_{c}", [P, PACK * (hi - lo)], BF16) for c, (lo, hi) in enumerate(spans)]
         yw = tile("yw", [P, S], I32)
         ys = tile("ys", [P, S], U8)
         out0_v = out_0.rearrange("(p t) n -> p t n", t=PACK)
         out1_v = out_1[0].rearrange("p c r -> p (c r)").bitcast(I32)
-
-        def members(c):
-            return mem_sb[:, 8 * c : 8 * c + 8]
 
         def weave(copy, dst, src):
             copy(
@@ -145,70 +135,78 @@ def tile_picked_bens8_relu_po_kernel(
                 src.rearrange("p t (c i) -> p c t i", i=4),
             )
 
+        def first_product(h, t):
+            acc = psum.tile([P, HALF], F32, name="acc1")
+            nc.tensor.matmul_mx(
+                out=acc[:],
+                lhsT=w1w[t][:].bitcast(FP8X4),
+                lhsT_scale=w1s[t][:],
+                rhs=xw[h][:].bitcast(FP8X4),
+                rhs_scale=xs[:, h * HALF : (h + 1) * HALF],
+                start=True,
+                stop=True,
+            )
+            nc.scalar.activation(hid[h, t], acc[:], RELU)
+            nc.vector.tensor_tensor(
+                z32[h][:, t, :], rin_sb[t][:].indirect(mem_sb[:, 16 * h : 16 * h + 16]), hid[h, t], MULT
+            )
+
         def round_hidden(c):
-            h, lo = divmod(c * CH, HALF)
-            weave(nc.scalar.copy, zbf[c][:], z32[h][:, :, lo : lo + CH])
+            lo, hi = spans[c]
+            h, base = divmod(lo, HALF)
+            weave(nc.scalar.copy, zbf[c][:], z32[h][:, :, base : base + hi - lo])
             nc.vector.quantize_mx(out=zw[c][:].bitcast(FP8X4), scales=zs[c][:], in_=zbf[c][:])
 
-        def second_product(c):
-            step = 2 if c == 0 else PACK
-            for lo in range(0, PACK, step):
-                acc = psum.tile([P, step, CH], F32, name="acc2")
-                for t in range(lo, lo + step):
-                    nc.tensor.matmul_mx(
-                        out=acc[:, t - lo, :],
-                        lhsT=w2w[:, 2 * P * t : 2 * P * (t + 1)].bitcast(FP4X4),
-                        lhsT_scale=w2s[:, P * t : P * t + P],
-                        rhs=zw[c][:].bitcast(FP8X4),
-                        rhs_scale=zs[c][:],
-                        start=True,
-                        stop=True,
-                    )
-                nc.scalar.copy(o32[c][:, lo : lo + step, :], acc[:])
+        def second_product(c, planes):
+            lo, hi = spans[c]
+            acc = psum.tile([P, len(planes), hi - lo], F32, name="acc2")
+            for i, t in enumerate(planes):
+                nc.tensor.matmul_mx(
+                    out=acc[:, i, :],
+                    lhsT=w2w[:, 2 * P * t : 2 * P * (t + 1)].bitcast(FP4X4),
+                    lhsT_scale=w2s[:, P * t : P * t + P],
+                    rhs=zw[c][:].bitcast(FP8X4),
+                    rhs_scale=zs[c][:],
+                    start=True,
+                    stop=True,
+                )
+            nc.scalar.copy(o32[c][:, planes[0] : planes[-1] + 1, :], acc[:])
+            for t in planes:
+                nc.vector.tensor_tensor(
+                    y32[c][:, t, :], so_sb[t][:].indirect(mem_sb[:, lo // 16 : hi // 16]), o32[c][:, t, :], MULT
+                )
 
-        def scale_output(c):
-            for t in range(PACK):
-                nc.vector.tensor_tensor(y32[c][:, t, :], so_sb[t][:].indirect(members(c)), o32[c][:, t, :], MULT)
-            nc.sync.dma_start(out0_v[:, :, c * CH : (c + 1) * CH], y32[c][:])
+        def store_output(c):
+            lo, hi = spans[c]
+            nc.sync.dma_start(out0_v[:, :, lo:hi], y32[c][:])
 
-        def round_output(copy, c, lo, hi):
-            h, base = divmod(c * CH, HALF)
-            weave(copy, ybf[h][:, PACK * (base + lo) : PACK * (base + hi)], y32[c][:, :, lo:hi])
+        def output_planes(c):
+            lo, hi = spans[c]
+            weave(nc.scalar.copy, ybf[c][:], y32[c][:])
+            nc.vector.quantize_mx(out=yw[:, lo:hi].bitcast(FP8X4), scales=ys[:, lo:hi], in_=ybf[c][:])
 
-        def output_planes(h):
-            cols = slice(h * HALF, (h + 1) * HALF)
-            nc.vector.quantize_mx(out=yw[:, cols].bitcast(FP8X4), scales=ys[:, cols], in_=ybf[h][:])
-            nc.sync.dma_start(out1_v[:, cols], yw[:, cols])
-
-        first_product(0, 0)
-        nc.vector.tensor_copy(
-            w2s[:].rearrange("p (t m) -> p t m", t=PACK), w2s_raw[:].rearrange("p (m t) -> p t m", t=PACK)
-        )
-        for t in range(1, PACK):
+        for t in range(PACK):
             first_product(0, t)
         for t in range(2):
             first_product(1, t)
         round_hidden(0)
-        first_product(1, 2)
+        for t in range(2, PACK):
+            first_product(1, t)
+        second_product(0, [0])
+        second_product(0, [1])
         round_hidden(1)
-        first_product(1, 3)
-        second_product(0)
-        scale_output(0)
+        second_product(0, [2])
         round_hidden(2)
-        second_product(1)
-        scale_output(1)
-        round_hidden(3)
-        second_product(2)
-        scale_output(2)
-        round_output(nc.scalar.copy, 0, 0, CH)
-        second_product(3)
-        scale_output(3)
-        round_output(nc.scalar.copy, 1, 0, CH)
-        round_output(nc.scalar.copy, 2, 0, CH)
-        round_output(nc.vector.tensor_copy, 3, 0, 96)
-        round_output(nc.scalar.copy, 3, 96, CH)
-        output_planes(0)
-        output_planes(1)
+        second_product(0, [3])
+        store_output(0)
+        for c in (1, 2):
+            second_product(c, [0, 1, 2, 3])
+            store_output(c)
+        for c in range(3):
+            output_planes(c)
+            if c == 1:
+                nc.sync.dma_start(out1_v[:, : HALF + CH], yw[:, : HALF + CH])
+        nc.sync.dma_start(out1_v[:, HALF + CH :], yw[:, HALF + CH :])
         for q in range(4):
             eng = nc.scalar if q % 2 else nc.sync
             eng.dma_start(out_2[0, 4 * q : 4 * q + 4, :].bitcast(I32), ys[32 * q : 32 * q + 4, :].bitcast(I32))

@@ -47,8 +47,8 @@ def tile_picked_bens8_relu_po_kernel(
         rin_sb = [tile(f"rin{t}", [P, W], F32) for t in range(PACK)]
         so_sb = [tile(f"so{t}", [P, W], F32) for t in range(PACK)]
 
-        nc.gpsimd.memset(xs_all[:].bitcast(I32), 0)
-        nc.gpsimd.memset(w2s_raw[:].bitcast(I32), 0)
+        nc.vector.memset(xs_all[:].bitcast(I32), 0)
+        nc.vector.memset(w2s_raw[:].bitcast(I32), 0)
 
         nc.sync.dma_start(offs_sb[:], offs)
         nc.sync.dma_start(w2w_raw[:].bitcast(I32), w2_words[0].bitcast(I32))
@@ -110,19 +110,17 @@ def tile_picked_bens8_relu_po_kernel(
         )
 
         z32 = [tile(f"z32_{h}", [P, PACK, HALF], F32) for h in range(2)]
-        hid_sb = tile("hid_sb", [P, 5, HALF], F32)
-        hid = {}
-        for t in range(3):
-            hid[0, t] = hid_sb[:, t, :]
-        hid[0, 3] = z32[1][:].rearrange("p t n -> p (t n)")[:, CH : CH + HALF]
+        hid_sb = tile("hid_sb", [P, 5 * HALF], F32)
+        starts = {(0, 0): 2 * HALF, (0, 1): 3 * HALF, (0, 2): CH, (0, 3): 4 * HALF}
         for t in range(PACK):
-            hid[1, t] = hid_sb[:, 3 + t % 2, :]
+            starts[1, t] = HALF * (t % 2)
+        hid = {key: hid_sb[:, lo : lo + HALF] for key, lo in starts.items()}
+        zbf = [tile(f"zbf_{h}", [P, PACK * HALF], BF16) for h in range(2)]
+        zw = [tile(f"zw_{h}", [P, HALF], I32) for h in range(2)]
+        zs = [tile(f"zs_{h}", [P, HALF], U8) for h in range(2)]
         spans = [(0, HALF), (HALF, HALF + CH), (HALF + CH, S)]
-        zbf = [tile(f"zbf_{c}", [P, PACK * (hi - lo)], BF16) for c, (lo, hi) in enumerate(spans)]
-        zw = [tile(f"zw_{c}", [P, hi - lo], I32) for c, (lo, hi) in enumerate(spans)]
-        zs = [tile(f"zs_{c}", [P, hi - lo], U8) for c, (lo, hi) in enumerate(spans)]
-        o32 = [tile(f"o32_{c}", [P, PACK, hi - lo], F32) for c, (lo, hi) in enumerate(spans)]
-        y32 = [tile(f"y32_{c}", [P, PACK, hi - lo], F32) for c, (lo, hi) in enumerate(spans)]
+        o32 = [tile(f"o32_{h}", [P, PACK, HALF], F32) for h in range(2)]
+        y32 = [tile(f"y32_{h}", [P, PACK, HALF], F32) for h in range(2)]
         ybf = [tile(f"ybf_{c}", [P, PACK * (hi - lo)], BF16) for c, (lo, hi) in enumerate(spans)]
         yw = tile("yw", [P, S], I32)
         ys = tile("ys", [P, S], U8)
@@ -151,38 +149,42 @@ def tile_picked_bens8_relu_po_kernel(
                 z32[h][:, t, :], rin_sb[t][:].indirect(mem_sb[:, 16 * h : 16 * h + 16]), hid[h, t], MULT
             )
 
-        def round_hidden(c):
-            lo, hi = spans[c]
-            h, base = divmod(lo, HALF)
-            weave(nc.scalar.copy, zbf[c][:], z32[h][:, :, base : base + hi - lo])
-            nc.vector.quantize_mx(out=zw[c][:].bitcast(FP8X4), scales=zs[c][:], in_=zbf[c][:])
+        def round_hidden(h):
+            weave(nc.scalar.copy, zbf[h][:], z32[h][:])
+            nc.vector.quantize_mx(out=zw[h][:].bitcast(FP8X4), scales=zs[h][:], in_=zbf[h][:])
 
-        def second_product(c, planes):
-            lo, hi = spans[c]
-            acc = psum.tile([P, len(planes), hi - lo], F32, name="acc2")
+        def second_product(h, planes):
+            acc = psum.tile([P, len(planes), HALF], F32, name="acc2")
             for i, t in enumerate(planes):
                 nc.tensor.matmul_mx(
                     out=acc[:, i, :],
                     lhsT=w2w[:, 2 * P * t : 2 * P * (t + 1)].bitcast(FP4X4),
                     lhsT_scale=w2s[:, P * t : P * t + P],
-                    rhs=zw[c][:].bitcast(FP8X4),
-                    rhs_scale=zs[c][:],
+                    rhs=zw[h][:].bitcast(FP8X4),
+                    rhs_scale=zs[h][:],
                     start=True,
                     stop=True,
                 )
-            nc.scalar.copy(o32[c][:, planes[0] : planes[-1] + 1, :], acc[:])
-            for t in planes:
-                nc.vector.tensor_tensor(
-                    y32[c][:, t, :], so_sb[t][:].indirect(mem_sb[:, lo // 16 : hi // 16]), o32[c][:, t, :], MULT
-                )
+            nc.scalar.copy(o32[h][:, planes[0] : planes[-1] + 1, :], acc[:])
 
-        def store_output(c):
+        def scale_output(t, lo, hi):
+            h, base = divmod(lo, HALF)
+            cols = slice(base, base + hi - lo)
+            nc.vector.tensor_tensor(
+                y32[h][:, t, cols], so_sb[t][:].indirect(mem_sb[:, lo // 16 : hi // 16]), o32[h][:, t, cols], MULT
+            )
+
+        def span_values(c):
             lo, hi = spans[c]
-            nc.sync.dma_start(out0_v[:, :, lo:hi], y32[c][:])
+            h, base = divmod(lo, HALF)
+            return y32[h][:, :, base : base + hi - lo]
+
+        def store_output(h, lo, hi):
+            nc.sync.dma_start(out0_v[:, lo:hi, h * HALF : (h + 1) * HALF], y32[h][:, lo:hi, :])
 
         def output_planes(c):
             lo, hi = spans[c]
-            weave(nc.scalar.copy, ybf[c][:], y32[c][:])
+            weave(nc.scalar.copy, ybf[c][:], span_values(c))
             nc.vector.quantize_mx(out=yw[:, lo:hi].bitcast(FP8X4), scales=ys[:, lo:hi], in_=ybf[c][:])
 
         for t in range(PACK):
@@ -192,16 +194,21 @@ def tile_picked_bens8_relu_po_kernel(
         round_hidden(0)
         for t in range(2, PACK):
             first_product(1, t)
-        second_product(0, [0])
-        second_product(0, [1])
-        round_hidden(1)
-        second_product(0, [2])
-        round_hidden(2)
-        second_product(0, [3])
-        store_output(0)
+        for t in range(PACK):
+            if t == 2:
+                round_hidden(1)
+            second_product(0, [t])
+            scale_output(t, 0, HALF)
+        store_output(0, 0, PACK)
+        for t in range(2):
+            second_product(1, [t])
+            scale_output(t, HALF, S)
+        store_output(1, 0, 2)
+        second_product(1, [2, 3])
         for c in (1, 2):
-            second_product(c, [0, 1, 2, 3])
-            store_output(c)
+            for t in (2, 3):
+                scale_output(t, *spans[c])
+        store_output(1, 2, PACK)
         for c in range(3):
             output_planes(c)
             if c == 1:

@@ -50,15 +50,21 @@ def tile_picked_bens8_relu_po_kernel(
         nc.vector.memset(xs_all[:].bitcast(I32), 0)
         nc.vector.memset(w2s_raw[:].bitcast(I32), 0)
 
+        warm = tile("warm", [P, 16], F32)
+        nc.gpsimd.memset(warm[:, :1], 0.0)
+        nc.scalar.activation(warm[:, 8:9], warm[:, :1], RELU)
+
         nc.sync.dma_start(offs_sb[:], offs)
         nc.sync.dma_start(w2w_raw[:].bitcast(I32), w2_words[0].bitcast(I32))
-        nc.sync.dma_start(w1_raw[:], w1.rearrange("(p j) c -> p j c", j=PACK))
+        w1_v = w1.rearrange("(p j) c -> p j c", j=PACK)
+        nc.sync.dma_start(w1_raw[:, :2, :], w1_v[:, :2, :])
         for q in range(4):
             nc.sync.dma_start(
                 xs_all[32 * q : 32 * q + 4, :].bitcast(I32), x_scales[0, 4 * q : 4 * q + 4, :].bitcast(I32)
             )
-        nc.sync.dma_start(xw_all[:], x_words[0].rearrange("p c r -> p (c r)").bitcast(I32))
+        nc.sync.dma_start(w1_raw[:, 2:, :], w1_v[:, 2:, :])
         nc.sync.dma_start(mem_sb[:], mem)
+        nc.sync.dma_start(xw_all[:], x_words[0].rearrange("p c r -> p (c r)").bitcast(I32))
         rin_v = rin.rearrange("(p t) u -> t p u", t=PACK)
         so_v = so.rearrange("(p t) u -> t p u", t=PACK)
         for q in range(4):
@@ -78,6 +84,7 @@ def tile_picked_bens8_relu_po_kernel(
         )
         xs = tile("xs", [P, S], U8)
 
+        nc.vector.tensor_copy(xs[:], xs_all[:].indirect(offs_sb[:]))
         w1_bf = tile("w1_bf", [P, PACK * W], BF16)
         w1_dst = w1_bf[:].rearrange("p (t m j) -> p m t j", t=PACK, j=PACK)
         w1_src = w1_raw[:].rearrange("p j (m t) -> p m t j", t=PACK)
@@ -87,10 +94,9 @@ def tile_picked_bens8_relu_po_kernel(
         def quantize_w1(t):
             nc.vector.quantize_mx(out=w1w[t][:].bitcast(FP8X4), scales=w1s[t][:], in_=w1_bf[:, W * t : W * (t + 1)])
 
-        split = 40
+        split = 80
         nc.scalar.copy(w1_dst[:, split:], w1_src[:, split:])
         nc.vector.tensor_copy(w1_dst[:, :split], w1_src[:, :split])
-        nc.vector.tensor_copy(xs[:], xs_all[:].indirect(offs_sb[:]))
         for t in range(2):
             quantize_w1(t)
 

@@ -41,21 +41,24 @@ def tile_picked_bens8_relu_po_kernel(
         mem_sb = tile("mem_sb", [P, S // 16], U16)
         xw_all = tile("xw_all", [P, T], I32)
         xs_all = tile("xs_all", [P, T], U8)
-        w1_raw = tile("w1_raw", [P, PACK, W], F32)
+        reuse = ctx.enter_context(tc.tile_pool(name="reuse", bufs=1))
+        w1_raw = reuse.tile([P, PACK, W], F32, name="w1_raw", offset=0)
         w2w_raw = tile("w2w_raw", [P, 2 * W], U8)
         w2s_raw = tile("w2s_raw", [P, W], U8)
         rin_sb = [tile(f"rin{t}", [P, W], F32) for t in range(PACK)]
-        so_sb = [tile(f"so{t}", [P, W], F32) for t in range(PACK)]
+        so_sb = [reuse.tile([P, W], F32, name=f"so{t}", offset=4 * W * t) for t in range(PACK)]
 
         nc.vector.memset(xs_all[:].bitcast(I32), 0)
         nc.vector.memset(w2s_raw[:].bitcast(I32), 0)
+        w2s = tile("w2s", [P, W], U8)
+        nc.vector.memset(w2s[:].bitcast(I32), 0)
 
         warm = tile("warm", [P, 16], F32)
         nc.gpsimd.memset(warm[:, :1], 0.0)
         nc.scalar.activation(warm[:, 8:9], warm[:, :1], RELU)
 
-        nc.sync.dma_start(offs_sb[:], offs)
         nc.sync.dma_start(w2w_raw[:].bitcast(I32), w2_words[0].bitcast(I32))
+        nc.sync.dma_start(offs_sb[:], offs)
         w1_v = w1.rearrange("(p j) c -> p j c", j=PACK)
         nc.sync.dma_start(w1_raw[:, :2, :], w1_v[:, :2, :])
         for q in range(4):
@@ -63,21 +66,16 @@ def tile_picked_bens8_relu_po_kernel(
                 xs_all[32 * q : 32 * q + 4, :].bitcast(I32), x_scales[0, 4 * q : 4 * q + 4, :].bitcast(I32)
             )
         nc.sync.dma_start(w1_raw[:, 2:, :], w1_v[:, 2:, :])
-        nc.sync.dma_start(mem_sb[:], mem)
+        nc.sync.dma_start(w2s_raw[:16, :].bitcast(I32), w2_scales[0].bitcast(I32))
         nc.sync.dma_start(xw_all[:], x_words[0].rearrange("p c r -> p (c r)").bitcast(I32))
+        nc.sync.dma_start(mem_sb[:], mem)
         rin_v = rin.rearrange("(p t) u -> t p u", t=PACK)
         so_v = so.rearrange("(p t) u -> t p u", t=PACK)
-        for q in range(4):
-            nc.sync.dma_start(
-                w2s_raw[32 * q : 32 * q + 4, :].bitcast(I32), w2_scales[0, 4 * q : 4 * q + 4, :].bitcast(I32)
-            )
         for t in range(PACK):
             nc.sync.dma_start(rin_sb[t][:], rin_v[t])
-        for t in range(PACK):
-            nc.sync.dma_start(so_sb[t][:], so_v[t])
 
         w2w = tile("w2w", [P, 2 * W], U8)
-        w2s = tile("w2s", [P, W], U8)
+        w2s_dealt = tile("w2s_dealt", [P, W], U8)
         nc.vector.tensor_copy(
             w2w[:].rearrange("p (t m b) -> p t m b", t=PACK, b=2),
             w2w_raw[:].rearrange("p (m t b) -> p t m b", t=PACK, b=2),
@@ -94,9 +92,16 @@ def tile_picked_bens8_relu_po_kernel(
         def quantize_w1(t):
             nc.vector.quantize_mx(out=w1w[t][:].bitcast(FP8X4), scales=w1s[t][:], in_=w1_bf[:, W * t : W * (t + 1)])
 
+        nc.vector.tensor_copy(
+            w2s_dealt[:].rearrange("p (t m) -> p t m", t=PACK), w2s_raw[:].rearrange("p (m t) -> p t m", t=PACK)
+        )
+        for q in range(4):
+            nc.sync.dma_start(w2s[32 * q : 32 * q + 4, :].bitcast(I32), w2s_dealt[4 * q : 4 * q + 4, :].bitcast(I32))
         split = 80
         nc.scalar.copy(w1_dst[:, split:], w1_src[:, split:])
         nc.vector.tensor_copy(w1_dst[:, :split], w1_src[:, :split])
+        for t in range(PACK):
+            nc.sync.dma_start(so_sb[t][:], so_v[t])
         for t in range(2):
             quantize_w1(t)
 
@@ -111,9 +116,6 @@ def tile_picked_bens8_relu_po_kernel(
         for t in range(2, PACK):
             quantize_w1(t)
         pick_words(1)
-        nc.vector.tensor_copy(
-            w2s[:].rearrange("p (t m) -> p t m", t=PACK), w2s_raw[:].rearrange("p (m t) -> p t m", t=PACK)
-        )
 
         z32 = [tile(f"z32_{h}", [P, PACK, HALF], F32) for h in range(2)]
         hid_sb = tile("hid_sb", [P, 5 * HALF], F32)
@@ -140,20 +142,27 @@ def tile_picked_bens8_relu_po_kernel(
             )
 
         def first_product(h, t):
-            acc = psum.tile([P, HALF], F32, name="acc1")
-            nc.tensor.matmul_mx(
-                out=acc[:],
-                lhsT=w1w[t][:].bitcast(FP8X4),
-                lhsT_scale=w1s[t][:],
-                rhs=xw[h][:].bitcast(FP8X4),
-                rhs_scale=xs[:, h * HALF : (h + 1) * HALF],
-                start=True,
-                stop=True,
-            )
-            nc.scalar.activation(hid[h, t], acc[:], RELU)
-            nc.vector.tensor_tensor(
-                z32[h][:, t, :], rin_sb[t][:].indirect(mem_sb[:, 16 * h : 16 * h + 16]), hid[h, t], MULT
-            )
+            step = CH if (h, t) == (0, 0) else HALF
+            for lo in range(0, HALF, step):
+                cols = slice(lo, lo + step)
+                first = h * HALF + lo
+                acc = psum.tile([P, step], F32, name="acc1")
+                nc.tensor.matmul_mx(
+                    out=acc[:],
+                    lhsT=w1w[t][:].bitcast(FP8X4),
+                    lhsT_scale=w1s[t][:],
+                    rhs=xw[h][:, cols].bitcast(FP8X4),
+                    rhs_scale=xs[:, first : first + step],
+                    start=True,
+                    stop=True,
+                )
+                nc.scalar.activation(hid[h, t][:, cols], acc[:], RELU)
+                nc.vector.tensor_tensor(
+                    z32[h][:, t, cols],
+                    rin_sb[t][:].indirect(mem_sb[:, first // 16 : (first + step) // 16]),
+                    hid[h, t][:, cols],
+                    MULT,
+                )
 
         def round_hidden(h):
             weave(nc.scalar.copy, zbf[h][:], z32[h][:])

@@ -53,10 +53,6 @@ def tile_picked_bens8_relu_po_kernel(
         w2s = tile("w2s", [P, W], U8)
         nc.vector.memset(w2s[:].bitcast(I32), 0)
 
-        warm = tile("warm", [P, 16], F32)
-        nc.gpsimd.memset(warm[:, :1], 0.0)
-        nc.scalar.activation(warm[:, 8:9], warm[:, :1], RELU)
-
         nc.sync.dma_start(w2w_raw[:].bitcast(I32), w2_words[0].bitcast(I32))
         nc.sync.dma_start(offs_sb[:], offs)
         w1_v = w1.rearrange("(p j) c -> p j c", j=PACK)
@@ -97,8 +93,9 @@ def tile_picked_bens8_relu_po_kernel(
         )
         for q in range(4):
             nc.sync.dma_start(w2s[32 * q : 32 * q + 4, :].bitcast(I32), w2s_dealt[4 * q : 4 * q + 4, :].bitcast(I32))
-        split = 80
-        nc.scalar.copy(w1_dst[:, split:], w1_src[:, split:])
+        split = 72
+        for j in (0, 2):
+            nc.scalar.copy(w1_dst[:, split:, :, j : j + 2], w1_src[:, split:, :, j : j + 2])
         nc.vector.tensor_copy(w1_dst[:, :split], w1_src[:, :split])
         for t in range(PACK):
             nc.sync.dma_start(so_sb[t][:], so_v[t])
@@ -118,11 +115,13 @@ def tile_picked_bens8_relu_po_kernel(
         pick_words(1)
 
         z32 = [tile(f"z32_{h}", [P, PACK, HALF], F32) for h in range(2)]
-        hid_sb = tile("hid_sb", [P, 5 * HALF], F32)
-        starts = {(0, 0): 2 * HALF, (0, 1): 3 * HALF, (0, 2): CH, (0, 3): 4 * HALF}
+        hid_sb = tile("hid_sb", [P, 5, HALF], F32)
+        hid = {}
+        for t in range(3):
+            hid[0, t] = hid_sb[:, t, :]
+        hid[0, 3] = z32[1][:].rearrange("p t n -> p (t n)")[:, CH : CH + HALF]
         for t in range(PACK):
-            starts[1, t] = HALF * (t % 2)
-        hid = {key: hid_sb[:, lo : lo + HALF] for key, lo in starts.items()}
+            hid[1, t] = hid_sb[:, 3 + t % 2, :]
         zbf = [tile(f"zbf_{h}", [P, PACK * HALF], BF16) for h in range(2)]
         zw = [tile(f"zw_{h}", [P, HALF], I32) for h in range(2)]
         zs = [tile(f"zs_{h}", [P, HALF], U8) for h in range(2)]
@@ -157,15 +156,20 @@ def tile_picked_bens8_relu_po_kernel(
                     stop=True,
                 )
                 nc.scalar.activation(hid[h, t][:, cols], acc[:], RELU)
-                nc.vector.tensor_tensor(
-                    z32[h][:, t, cols],
-                    rin_sb[t][:].indirect(mem_sb[:, first // 16 : (first + step) // 16]),
-                    hid[h, t][:, cols],
-                    MULT,
-                )
+                piece = CH if (h, t) == (0, PACK - 1) else step
+                for at in range(lo, lo + step, piece):
+                    entry = h * HALF + at
+                    nc.vector.tensor_tensor(
+                        z32[h][:, t, at : at + piece],
+                        rin_sb[t][:].indirect(mem_sb[:, entry // 16 : (entry + piece) // 16]),
+                        hid[h, t][:, at : at + piece],
+                        MULT,
+                    )
 
         def round_hidden(h):
-            weave(nc.scalar.copy, zbf[h][:], z32[h][:])
+            step = CH if h == 0 else HALF
+            for lo in range(0, HALF, step):
+                weave(nc.scalar.copy, zbf[h][:, PACK * lo : PACK * (lo + step)], z32[h][:, :, lo : lo + step])
             nc.vector.quantize_mx(out=zw[h][:].bitcast(FP8X4), scales=zs[h][:], in_=zbf[h][:])
 
         def second_product(h, planes):

@@ -32,7 +32,7 @@ def tile_picked_bens8_relu_po_kernel(
     nc = tc.nc
     with ExitStack() as ctx:
         keep = ctx.enter_context(tc.tile_pool(name="keep", bufs=1))
-        psum = ctx.enter_context(tc.psum_pool(name="psum", bufs=4))
+        psum = ctx.enter_context(tc.psum_pool(name="psum", bufs=1))
 
         def tile(name, shape, dtype):
             return keep.tile(shape, dtype, name=name, align_bytes=64)
@@ -41,150 +41,136 @@ def tile_picked_bens8_relu_po_kernel(
         mem_sb = tile("mem_sb", [P, S // 16], U16)
         xw_all = tile("xw_all", [P, T], I32)
         xs_all = tile("xs_all", [P, T], U8)
-        reuse = ctx.enter_context(tc.tile_pool(name="reuse", bufs=1))
-        w1_raw = reuse.tile([P, PACK, W], F32, name="w1_raw", offset=0)
+        xs_picked = tile("xs_picked", [P, S], U8)
+        xs = tile("xs", [P, S], U8)
+        w1_raw = tile("w1_raw", [P, PACK, W], F32)
         w2w_raw = tile("w2w_raw", [P, 2 * W], U8)
         w2s_raw = tile("w2s_raw", [P, W], U8)
+        w2w = tile("w2w", [P, 2 * W], U8)
+        w2s_dealt = tile("w2s_dealt", [P, W], U8)
+        w2s = tile("w2s", [P, W], U8)
         rin_sb = [tile(f"rin{t}", [P, W], F32) for t in range(PACK)]
-        so_sb = [reuse.tile([P, W], F32, name=f"so{t}", offset=4 * W * t) for t in range(PACK)]
+        so_sb = [tile(f"so{t}", [P, W], F32) for t in range(PACK)]
 
         nc.vector.memset(xs_all[:].bitcast(I32), 0)
         nc.vector.memset(w2s_raw[:].bitcast(I32), 0)
-        w2s = tile("w2s", [P, W], U8)
+        nc.vector.memset(xs[:].bitcast(I32), 0)
         nc.vector.memset(w2s[:].bitcast(I32), 0)
 
-        nc.sync.dma_start(w2w_raw[:].bitcast(I32), w2_words[0].bitcast(I32))
-        nc.sync.dma_start(offs_sb[:], offs)
-        w1_v = w1.rearrange("(p j) c -> p j c", j=PACK)
-        nc.sync.dma_start(w1_raw[:, :2, :], w1_v[:, :2, :])
-        for q in range(4):
-            nc.sync.dma_start(
-                xs_all[32 * q : 32 * q + 4, :].bitcast(I32), x_scales[0, 4 * q : 4 * q + 4, :].bitcast(I32)
-            )
-        nc.sync.dma_start(w1_raw[:, 2:, :], w1_v[:, 2:, :])
-        nc.sync.dma_start(w2s_raw[:16, :].bitcast(I32), w2_scales[0].bitcast(I32))
-        nc.sync.dma_start(xw_all[:], x_words[0].rearrange("p c r -> p (c r)").bitcast(I32))
-        nc.sync.dma_start(mem_sb[:], mem)
         rin_v = rin.rearrange("(p t) u -> t p u", t=PACK)
         so_v = so.rearrange("(p t) u -> t p u", t=PACK)
-        for t in range(PACK):
-            nc.sync.dma_start(rin_sb[t][:], rin_v[t])
+        w1_v = w1.rearrange("(p j) c -> p j c", j=PACK)
+        nc.sync.dma_start(rin_sb[0][:], rin_v[0])
+        nc.sync.dma_start(mem_sb[:], mem)
+        nc.sync.dma_start(offs_sb[:], offs)
+        nc.sync.dma_start(xs_all[0:P:8, :].bitcast(I32), x_scales[0].bitcast(I32))
+        nc.sync.dma_start(w1_raw[:, :2, :], w1_v[:, :2, :])
+        nc.sync.dma_start(rin_sb[1][:], rin_v[1])
+        nc.sync.dma_start(w1_raw[:, 2:, :], w1_v[:, 2:, :])
+        nc.sync.dma_start(rin_sb[2][:], rin_v[2])
+        nc.sync.dma_start(w2w_raw[:].bitcast(I32), w2_words[0].bitcast(I32))
+        nc.sync.dma_start(rin_sb[3][:], rin_v[3])
+        nc.sync.dma_start(w2s_raw[:16, :].bitcast(I32), w2_scales[0].bitcast(I32))
+        nc.sync.dma_start(xw_all[:], x_words[0].rearrange("p c r -> p (c r)").bitcast(I32))
 
-        w2w = tile("w2w", [P, 2 * W], U8)
-        w2s_dealt = tile("w2s_dealt", [P, W], U8)
-        nc.vector.tensor_copy(
+        nc.vector.tensor_copy(xs_picked[:], xs_all[:].indirect(offs_sb[:]))
+        for q in range(4):
+            nc.sync.dma_start(
+                xs[32 * q : 32 * q + 4, :].bitcast(I32), xs_picked[32 * q : 32 * q + 32 : 8, :].bitcast(I32)
+            )
+        for t in range(PACK):
+            nc.sync.dma_start(so_sb[t][:], so_v[t])
+
+        nc.gpsimd.tensor_copy(
             w2w[:].rearrange("p (t m b) -> p t m b", t=PACK, b=2),
             w2w_raw[:].rearrange("p (m t b) -> p t m b", t=PACK, b=2),
         )
-        xs = tile("xs", [P, S], U8)
-
-        nc.vector.tensor_copy(xs[:], xs_all[:].indirect(offs_sb[:]))
-        w1_bf = tile("w1_bf", [P, PACK * W], BF16)
-        w1_dst = w1_bf[:].rearrange("p (t m j) -> p m t j", t=PACK, j=PACK)
-        w1_src = w1_raw[:].rearrange("p j (m t) -> p m t j", t=PACK)
-        w1w = [tile(f"w1w{t}", [P, P], I32) for t in range(PACK)]
-        w1s = [tile(f"w1s{t}", [P, P], U8) for t in range(PACK)]
-
-        def quantize_w1(t):
-            nc.vector.quantize_mx(out=w1w[t][:].bitcast(FP8X4), scales=w1s[t][:], in_=w1_bf[:, W * t : W * (t + 1)])
-
-        nc.vector.tensor_copy(
+        nc.gpsimd.tensor_copy(
             w2s_dealt[:].rearrange("p (t m) -> p t m", t=PACK), w2s_raw[:].rearrange("p (m t) -> p t m", t=PACK)
         )
         for q in range(4):
             nc.sync.dma_start(w2s[32 * q : 32 * q + 4, :].bitcast(I32), w2s_dealt[4 * q : 4 * q + 4, :].bitcast(I32))
-        split = 72
-        for j in (0, 2):
-            nc.scalar.copy(w1_dst[:, split:, :, j : j + 2], w1_src[:, split:, :, j : j + 2])
-        nc.vector.tensor_copy(w1_dst[:, :split], w1_src[:, :split])
+
+        fac = [tile(f"fac{h}", [P, PACK, HALF], F32) for h in range(2)]
         for t in range(PACK):
-            nc.sync.dma_start(so_sb[t][:], so_v[t])
-        for t in range(2):
-            quantize_w1(t)
+            for h in range(2):
+                nc.vector.tensor_copy(fac[h][:, t, :], rin_sb[t][:].indirect(mem_sb[:, 16 * h : 16 * h + 16]))
+
+        w1_bf = tile("w1_bf", [P, PACK * W], BF16)
+        w1_dst = w1_bf[:].rearrange("p (t m j) -> p m t j", t=PACK, j=PACK)
+        w1_src = w1_raw[:].rearrange("p j (m t) -> p m t j", t=PACK)
+        for j in (0, 2):
+            nc.scalar.copy(w1_dst[:, :, :, j : j + 2], w1_src[:, :, :, j : j + 2])
+        w1w = tile("w1w", [P, W], I32)
+        w1s = tile("w1s", [P, W], U8)
+        nc.vector.quantize_mx(out=w1w[:].bitcast(FP8X4), scales=w1s[:], in_=w1_bf[:])
 
         xw = [tile(f"xw{h}", [P, HALF], I32) for h in range(2)]
-
-        def pick_words(h):
+        for h in (1, 0):
             nc.vector.tensor_copy(
                 xw[h][:].bitcast(U32), xw_all[:].bitcast(U32).indirect(offs_sb[:, 16 * h : 16 * h + 16])
             )
 
-        pick_words(0)
-        for t in range(2, PACK):
-            quantize_w1(t)
-        pick_words(1)
-
-        z32 = [tile(f"z32_{h}", [P, PACK, HALF], F32) for h in range(2)]
-        hid_sb = tile("hid_sb", [P, 5, HALF], F32)
-        hid = {}
-        for t in range(3):
-            hid[0, t] = hid_sb[:, t, :]
-        hid[0, 3] = z32[1][:].rearrange("p t n -> p (t n)")[:, CH : CH + HALF]
-        for t in range(PACK):
-            hid[1, t] = hid_sb[:, 3 + t % 2, :]
+        hid = tile("hid", [P, PACK, CH], F32)
+        z32 = [tile(f"z32_{c}", [P, PACK, CH], F32) for c in range(NCH)]
         zbf = [tile(f"zbf_{h}", [P, PACK * HALF], BF16) for h in range(2)]
         zw = [tile(f"zw_{h}", [P, HALF], I32) for h in range(2)]
         zs = [tile(f"zs_{h}", [P, HALF], U8) for h in range(2)]
-        spans = [(0, HALF), (HALF, HALF + CH), (HALF + CH, S)]
         o32 = [tile(f"o32_{h}", [P, PACK, HALF], F32) for h in range(2)]
         y32 = [tile(f"y32_{h}", [P, PACK, HALF], F32) for h in range(2)]
-        ybf = [tile(f"ybf_{c}", [P, PACK * (hi - lo)], BF16) for c, (lo, hi) in enumerate(spans)]
+        spans = [(0, HALF), (HALF, HALF + CH), (HALF + CH, S)]
+        ybf = [tile(f"ybf_{i}", [P, PACK * (hi - lo)], BF16) for i, (lo, hi) in enumerate(spans)]
         yw = tile("yw", [P, S], I32)
         ys = tile("ys", [P, S], U8)
         out0_v = out_0.rearrange("(p t) n -> p t n", t=PACK)
         out1_v = out_1[0].rearrange("p c r -> p (c r)").bitcast(I32)
 
-        def weave(copy, dst, src):
-            copy(
-                dst.rearrange("p (c i t) -> p c t i", i=4, t=PACK),
-                src.rearrange("p t (c i) -> p c t i", i=4),
+        def weave(dst, src):
+            nc.scalar.copy(
+                dst.rearrange("p (c i t) -> p c t i", i=4, t=PACK), src.rearrange("p t (c i) -> p c t i", i=4)
             )
 
-        def first_product(h, t):
-            step = CH if (h, t) == (0, 0) else HALF
-            for lo in range(0, HALF, step):
-                cols = slice(lo, lo + step)
-                first = h * HALF + lo
-                acc = psum.tile([P, step], F32, name="acc1")
+        def hidden(c):
+            h, base = divmod(c * CH, HALF)
+            acc = psum.tile([P, PACK, CH], F32, name=f"acc1_{c}")
+            for t in range(PACK):
                 nc.tensor.matmul_mx(
-                    out=acc[:],
-                    lhsT=w1w[t][:].bitcast(FP8X4),
-                    lhsT_scale=w1s[t][:],
-                    rhs=xw[h][:, cols].bitcast(FP8X4),
-                    rhs_scale=xs[:, first : first + step],
+                    out=acc[:, t, :],
+                    lhsT=w1w[:, P * t : P * (t + 1)].bitcast(FP8X4),
+                    lhsT_scale=w1s[:, P * t : P * (t + 1)],
+                    rhs=xw[h][:, base : base + CH].bitcast(FP8X4),
+                    rhs_scale=xs[:, c * CH : (c + 1) * CH],
                     start=True,
                     stop=True,
                 )
-                nc.scalar.activation(hid[h, t][:, cols], acc[:], RELU)
-                piece = CH if (h, t) == (0, PACK - 1) else step
-                for at in range(lo, lo + step, piece):
-                    entry = h * HALF + at
-                    nc.vector.tensor_tensor(
-                        z32[h][:, t, at : at + piece],
-                        rin_sb[t][:].indirect(mem_sb[:, entry // 16 : (entry + piece) // 16]),
-                        hid[h, t][:, at : at + piece],
-                        MULT,
-                    )
+            factors = fac[h][:, :, base : base + CH]
+            if c == NCH - 1:
+                nc.scalar.activation(hid[:], acc[:], RELU)
+                nc.gpsimd.tensor_tensor(z32[c][:], hid[:], factors, MULT)
+            else:
+                nc.vector.scalar_tensor_tensor(z32[c][:], acc[:], 0.0, factors, MAX, MULT)
 
-        def round_hidden(h):
-            step = CH if h == 0 else HALF
-            for lo in range(0, HALF, step):
-                weave(nc.scalar.copy, zbf[h][:, PACK * lo : PACK * (lo + step)], z32[h][:, :, lo : lo + step])
+        def round_hidden(c):
+            h, base = divmod(c * CH, HALF)
+            weave(zbf[h][:, PACK * base : PACK * (base + CH)], z32[c][:])
+
+        def quantize_hidden(h):
             nc.vector.quantize_mx(out=zw[h][:].bitcast(FP8X4), scales=zs[h][:], in_=zbf[h][:])
 
-        def second_product(h, planes):
-            acc = psum.tile([P, len(planes), HALF], F32, name="acc2")
-            for i, t in enumerate(planes):
+        def second_product(h, pair):
+            acc = psum.tile([P, 2, HALF], F32, name=f"acc2_{h}_{pair}")
+            for i in range(2):
+                t = 2 * pair + i
                 nc.tensor.matmul_mx(
                     out=acc[:, i, :],
                     lhsT=w2w[:, 2 * P * t : 2 * P * (t + 1)].bitcast(FP4X4),
-                    lhsT_scale=w2s[:, P * t : P * t + P],
+                    lhsT_scale=w2s[:, P * t : P * (t + 1)],
                     rhs=zw[h][:].bitcast(FP8X4),
                     rhs_scale=zs[h][:],
                     start=True,
                     stop=True,
                 )
-            nc.scalar.copy(o32[h][:, planes[0] : planes[-1] + 1, :], acc[:])
+            return acc
 
         def scale_output(t, lo, hi):
             h, base = divmod(lo, HALF)
@@ -193,44 +179,47 @@ def tile_picked_bens8_relu_po_kernel(
                 y32[h][:, t, cols], so_sb[t][:].indirect(mem_sb[:, lo // 16 : hi // 16]), o32[h][:, t, cols], MULT
             )
 
-        def span_values(c):
-            lo, hi = spans[c]
-            h, base = divmod(lo, HALF)
-            return y32[h][:, :, base : base + hi - lo]
-
         def store_output(h, lo, hi):
             nc.sync.dma_start(out0_v[:, lo:hi, h * HALF : (h + 1) * HALF], y32[h][:, lo:hi, :])
 
-        def output_planes(c):
-            lo, hi = spans[c]
-            weave(nc.scalar.copy, ybf[c][:], span_values(c))
-            nc.vector.quantize_mx(out=yw[:, lo:hi].bitcast(FP8X4), scales=ys[:, lo:hi], in_=ybf[c][:])
+        def output_planes(i):
+            lo, hi = spans[i]
+            h, base = divmod(lo, HALF)
+            weave(ybf[i][:], y32[h][:, :, base : base + hi - lo])
+            nc.vector.quantize_mx(out=yw[:, lo:hi].bitcast(FP8X4), scales=ys[:, lo:hi], in_=ybf[i][:])
 
-        for t in range(PACK):
-            first_product(0, t)
+        early = tile("early", [P, HALF], F32)
+        ahead = [early[:], fac[0][:, 0, :]]
+        nc.vector.tensor_copy(ahead[0], so_sb[0][:].indirect(mem_sb[:, :16]))
+        hidden(3)
+        for c in range(2):
+            hidden(c)
+            round_hidden(c)
+        hidden(2)
+        quantize_hidden(0)
+        nc.vector.tensor_copy(ahead[1], so_sb[1][:].indirect(mem_sb[:, :16]))
+        round_hidden(2)
+        round_hidden(3)
+        first = second_product(0, 0)
+        nc.scalar.copy(o32[0][:, 2:, :], second_product(0, 1)[:])
+        quantize_hidden(1)
         for t in range(2):
-            first_product(1, t)
-        round_hidden(0)
+            nc.vector.tensor_tensor(y32[0][:, t, :], first[:, t, :], ahead[t], MULT)
         for t in range(2, PACK):
-            first_product(1, t)
-        for t in range(PACK):
-            if t == 2:
-                round_hidden(1)
-            second_product(0, [t])
             scale_output(t, 0, HALF)
         store_output(0, 0, PACK)
+        for pair in range(2):
+            nc.scalar.copy(o32[1][:, 2 * pair : 2 * pair + 2, :], second_product(1, pair)[:])
         for t in range(2):
-            second_product(1, [t])
             scale_output(t, HALF, S)
         store_output(1, 0, 2)
-        second_product(1, [2, 3])
-        for c in (1, 2):
+        for i in (1, 2):
             for t in (2, 3):
-                scale_output(t, *spans[c])
+                scale_output(t, *spans[i])
         store_output(1, 2, PACK)
-        for c in range(3):
-            output_planes(c)
-            if c == 1:
+        for i in range(3):
+            output_planes(i)
+            if i == 1:
                 nc.sync.dma_start(out1_v[:, : HALF + CH], yw[:, : HALF + CH])
         nc.sync.dma_start(out1_v[:, HALF + CH :], yw[:, HALF + CH :])
         for q in range(4):

@@ -34,6 +34,10 @@ def tile_picked_bens8_relu_po_kernel(
         keep = ctx.enter_context(tc.tile_pool(name="keep", bufs=1))
         psum = ctx.enter_context(tc.psum_pool(name="psum", bufs=1))
 
+        reuse = ctx.enter_context(tc.tile_pool(name="reuse", bufs=1))
+
+        psum2 = ctx.enter_context(tc.psum_pool(name="psum2", bufs=4))
+
         def tile(name, shape, dtype):
             return keep.tile(shape, dtype, name=name, align_bytes=64)
 
@@ -69,7 +73,6 @@ def tile_picked_bens8_relu_po_kernel(
         nc.sync.dma_start(w1_raw[:, 2:, :], w1_v[:, 2:, :])
         nc.sync.dma_start(rin_sb[2][:], rin_v[2])
         nc.sync.dma_start(w2w_raw[:].bitcast(I32), w2_words[0].bitcast(I32))
-        nc.sync.dma_start(rin_sb[3][:], rin_v[3])
         nc.sync.dma_start(w2s_raw[:16, :].bitcast(I32), w2_scales[0].bitcast(I32))
         nc.sync.dma_start(xw_all[:], x_words[0].rearrange("p c r -> p (c r)").bitcast(I32))
 
@@ -78,6 +81,7 @@ def tile_picked_bens8_relu_po_kernel(
             nc.sync.dma_start(
                 xs[32 * q : 32 * q + 4, :].bitcast(I32), xs_picked[32 * q : 32 * q + 32 : 8, :].bitcast(I32)
             )
+        nc.sync.dma_start(rin_sb[3][:], rin_v[3])
         for t in range(PACK):
             nc.sync.dma_start(so_sb[t][:], so_v[t])
 
@@ -92,9 +96,13 @@ def tile_picked_bens8_relu_po_kernel(
             nc.sync.dma_start(w2s[32 * q : 32 * q + 4, :].bitcast(I32), w2s_dealt[4 * q : 4 * q + 4, :].bitcast(I32))
 
         fac = [tile(f"fac{h}", [P, PACK, HALF], F32) for h in range(2)]
-        for t in range(PACK):
+
+        def pick_input_factors(h, t):
+            nc.vector.tensor_copy(fac[h][:, t, :], rin_sb[t][:].indirect(mem_sb[:, 16 * h : 16 * h + 16]))
+
+        for t in range(PACK - 1):
             for h in range(2):
-                nc.vector.tensor_copy(fac[h][:, t, :], rin_sb[t][:].indirect(mem_sb[:, 16 * h : 16 * h + 16]))
+                pick_input_factors(h, t)
 
         w1_bf = tile("w1_bf", [P, PACK * W], BF16)
         w1_dst = w1_bf[:].rearrange("p (t m j) -> p m t j", t=PACK, j=PACK)
@@ -106,15 +114,18 @@ def tile_picked_bens8_relu_po_kernel(
         nc.vector.quantize_mx(out=w1w[:].bitcast(FP8X4), scales=w1s[:], in_=w1_bf[:])
 
         xw = [tile(f"xw{h}", [P, HALF], I32) for h in range(2)]
-        for h in (1, 0):
+        for h in range(2):
             nc.vector.tensor_copy(
                 xw[h][:].bitcast(U32), xw_all[:].bitcast(U32).indirect(offs_sb[:, 16 * h : 16 * h + 16])
             )
 
-        hid = tile("hid", [P, PACK, CH], F32)
+        hid = reuse.tile([P, PACK, CH], F32, name="hid", offset=4096, align_bytes=64)
         z32 = [tile(f"z32_{c}", [P, PACK, CH], F32) for c in range(NCH)]
-        zbf = [tile(f"zbf_{h}", [P, PACK * HALF], BF16) for h in range(2)]
-        zw = [tile(f"zw_{h}", [P, HALF], I32) for h in range(2)]
+        zbf = [
+            reuse.tile([P, PACK * HALF], BF16, name=f"zbf_{h}", offset=2 * PACK * HALF * h, align_bytes=64)
+            for h in range(2)
+        ]
+        zw = [tile("zw_0", [P, HALF], I32), reuse.tile([P, HALF], I32, name="zw_1", offset=4096, align_bytes=64)]
         zs = [tile(f"zs_{h}", [P, HALF], U8) for h in range(2)]
         o32 = [tile(f"o32_{h}", [P, PACK, HALF], F32) for h in range(2)]
         y32 = [tile(f"y32_{h}", [P, PACK, HALF], F32) for h in range(2)]
@@ -125,10 +136,14 @@ def tile_picked_bens8_relu_po_kernel(
         out0_v = out_0.rearrange("(p t) n -> p t n", t=PACK)
         out1_v = out_1[0].rearrange("p c r -> p (c r)").bitcast(I32)
 
-        def weave(dst, src):
-            nc.scalar.copy(
-                dst.rearrange("p (c i t) -> p c t i", i=4, t=PACK), src.rearrange("p t (c i) -> p c t i", i=4)
-            )
+        def woven(ap):
+            return ap.rearrange("p (c i t) -> p c t i", i=4, t=PACK)
+
+        def by_planes(ap):
+            return ap.rearrange("p t (c i) -> p c t i", i=4)
+
+        def weave(copy, dst, src):
+            copy(woven(dst), by_planes(src))
 
         def hidden(c):
             h, base = divmod(c * CH, HALF)
@@ -144,23 +159,24 @@ def tile_picked_bens8_relu_po_kernel(
                     stop=True,
                 )
             factors = fac[h][:, :, base : base + CH]
-            if c == NCH - 1:
+            if c == 1:
                 nc.scalar.activation(hid[:], acc[:], RELU)
-                nc.gpsimd.tensor_tensor(z32[c][:], hid[:], factors, MULT)
+                nc.gpsimd.tensor_tensor(
+                    woven(zbf[h][:, PACK * base : PACK * (base + CH)]), by_planes(hid[:]), by_planes(factors), MULT
+                )
             else:
                 nc.vector.scalar_tensor_tensor(z32[c][:], acc[:], 0.0, factors, MAX, MULT)
 
         def round_hidden(c):
             h, base = divmod(c * CH, HALF)
-            weave(zbf[h][:, PACK * base : PACK * (base + CH)], z32[c][:])
+            weave(nc.scalar.copy, zbf[h][:, PACK * base : PACK * (base + CH)], z32[c][:])
 
         def quantize_hidden(h):
             nc.vector.quantize_mx(out=zw[h][:].bitcast(FP8X4), scales=zs[h][:], in_=zbf[h][:])
 
-        def second_product(h, pair):
-            acc = psum.tile([P, 2, HALF], F32, name=f"acc2_{h}_{pair}")
-            for i in range(2):
-                t = 2 * pair + i
+        def second_product(h, planes):
+            acc = psum2.tile([P, len(planes), HALF], F32, name="acc2")
+            for i, t in enumerate(planes):
                 nc.tensor.matmul_mx(
                     out=acc[:, i, :],
                     lhsT=w2w[:, 2 * P * t : 2 * P * (t + 1)].bitcast(FP4X4),
@@ -185,31 +201,34 @@ def tile_picked_bens8_relu_po_kernel(
         def output_planes(i):
             lo, hi = spans[i]
             h, base = divmod(lo, HALF)
-            weave(ybf[i][:], y32[h][:, :, base : base + hi - lo])
+            cut = 48 if i == len(spans) - 1 else hi - lo
+            weave(nc.scalar.copy, ybf[i][:, : PACK * cut], y32[h][:, :, base : base + cut])
+            if cut < hi - lo:
+                weave(nc.vector.tensor_copy, ybf[i][:, PACK * cut :], y32[h][:, :, base + cut : base + hi - lo])
             nc.vector.quantize_mx(out=yw[:, lo:hi].bitcast(FP8X4), scales=ys[:, lo:hi], in_=ybf[i][:])
 
-        early = tile("early", [P, HALF], F32)
-        ahead = [early[:], fac[0][:, 0, :]]
-        nc.vector.tensor_copy(ahead[0], so_sb[0][:].indirect(mem_sb[:, :16]))
-        hidden(3)
-        for c in range(2):
+        ahead = reuse.tile([P, HALF], F32, name="ahead", offset=0, align_bytes=64)
+        pick_input_factors(0, PACK - 1)
+        hidden(1)
+        hidden(0)
+        round_hidden(0)
+        pick_input_factors(1, PACK - 1)
+        for c in (2, 3):
             hidden(c)
-            round_hidden(c)
-        hidden(2)
         quantize_hidden(0)
-        nc.vector.tensor_copy(ahead[1], so_sb[1][:].indirect(mem_sb[:, :16]))
-        round_hidden(2)
-        round_hidden(3)
-        first = second_product(0, 0)
-        nc.scalar.copy(o32[0][:, 2:, :], second_product(0, 1)[:])
+        nc.vector.tensor_copy(ahead[:], so_sb[0][:].indirect(mem_sb[:, :16]))
+        for c in (2, 3):
+            round_hidden(c)
+        nc.scalar.copy(o32[0][:, 1, :], second_product(0, [1])[:, 0, :])
+        first = second_product(0, [0])
+        nc.scalar.copy(o32[0][:, 2:, :], second_product(0, [2, 3])[:])
         quantize_hidden(1)
-        for t in range(2):
-            nc.vector.tensor_tensor(y32[0][:, t, :], first[:, t, :], ahead[t], MULT)
-        for t in range(2, PACK):
+        nc.vector.tensor_tensor(y32[0][:, 0, :], first[:, 0, :], ahead[:], MULT)
+        for t in range(1, PACK):
             scale_output(t, 0, HALF)
         store_output(0, 0, PACK)
         for pair in range(2):
-            nc.scalar.copy(o32[1][:, 2 * pair : 2 * pair + 2, :], second_product(1, pair)[:])
+            nc.scalar.copy(o32[1][:, 2 * pair : 2 * pair + 2, :], second_product(1, [2 * pair, 2 * pair + 1])[:])
         for t in range(2):
             scale_output(t, HALF, S)
         store_output(1, 0, 2)

@@ -72,7 +72,6 @@ def tile_picked_bens8_relu_po_kernel(
         nc.sync.dma_start(rin_sb[1][:], rin_v[1])
         nc.sync.dma_start(w1_raw[:, 2:, :], w1_v[:, 2:, :])
         nc.sync.dma_start(rin_sb[2][:], rin_v[2])
-        nc.sync.dma_start(w2w_raw[:].bitcast(I32), w2_words[0].bitcast(I32))
         nc.sync.dma_start(w2s_raw[:16, :].bitcast(I32), w2_scales[0].bitcast(I32))
         nc.sync.dma_start(xw_all[:], x_words[0].rearrange("p c r -> p (c r)").bitcast(I32))
 
@@ -81,16 +80,17 @@ def tile_picked_bens8_relu_po_kernel(
             nc.sync.dma_start(
                 xs[32 * q : 32 * q + 4, :].bitcast(I32), xs_picked[32 * q : 32 * q + 32 : 8, :].bitcast(I32)
             )
+        nc.sync.dma_start(w2w_raw[:].bitcast(I32), w2_words[0].bitcast(I32))
         nc.sync.dma_start(rin_sb[3][:], rin_v[3])
         for t in range(PACK):
             nc.sync.dma_start(so_sb[t][:], so_v[t])
 
         nc.gpsimd.tensor_copy(
-            w2w[:].rearrange("p (t m b) -> p t m b", t=PACK, b=2),
-            w2w_raw[:].rearrange("p (m t b) -> p t m b", t=PACK, b=2),
+            w2s_dealt[:].rearrange("p (t m) -> p t m", t=PACK), w2s_raw[:].rearrange("p (m t) -> p t m", t=PACK)
         )
         nc.gpsimd.tensor_copy(
-            w2s_dealt[:].rearrange("p (t m) -> p t m", t=PACK), w2s_raw[:].rearrange("p (m t) -> p t m", t=PACK)
+            w2w[:].rearrange("p (t m b) -> p t m b", t=PACK, b=2),
+            w2w_raw[:].rearrange("p (m t b) -> p t m b", t=PACK, b=2),
         )
         for q in range(4):
             nc.sync.dma_start(w2s[32 * q : 32 * q + 4, :].bitcast(I32), w2s_dealt[4 * q : 4 * q + 4, :].bitcast(I32))

@@ -145,12 +145,12 @@ def tile_picked_bens8_relu_po_kernel(
         def weave(copy, dst, src):
             copy(woven(dst), by_planes(src))
 
-        def hidden(c):
+        def first_product(c, planes, pool, name):
             h, base = divmod(c * CH, HALF)
-            acc = psum.tile([P, PACK, CH], F32, name=f"acc1_{c}")
-            for t in range(PACK):
+            acc = pool.tile([P, len(planes), CH], F32, name=name)
+            for i, t in enumerate(planes):
                 nc.tensor.matmul_mx(
-                    out=acc[:, t, :],
+                    out=acc[:, i, :],
                     lhsT=w1w[:, P * t : P * (t + 1)].bitcast(FP8X4),
                     lhsT_scale=w1s[:, P * t : P * (t + 1)],
                     rhs=xw[h][:, base : base + CH].bitcast(FP8X4),
@@ -158,13 +158,19 @@ def tile_picked_bens8_relu_po_kernel(
                     start=True,
                     stop=True,
                 )
+            return acc
+
+        def hidden(c):
+            h, base = divmod(c * CH, HALF)
             factors = fac[h][:, :, base : base + CH]
             if c == 1:
-                nc.scalar.activation(hid[:], acc[:], RELU)
+                for lo in (0, 2):
+                    nc.scalar.activation(hid[:, lo : lo + 2, :], first_product(c, [lo, lo + 1], psum2, "acc2")[:], RELU)
                 nc.gpsimd.tensor_tensor(
                     woven(zbf[h][:, PACK * base : PACK * (base + CH)]), by_planes(hid[:]), by_planes(factors), MULT
                 )
             else:
+                acc = first_product(c, range(PACK), psum, f"acc1_{c}")
                 nc.vector.scalar_tensor_tensor(z32[c][:], acc[:], 0.0, factors, MAX, MULT)
 
         def round_hidden(c):
@@ -207,7 +213,7 @@ def tile_picked_bens8_relu_po_kernel(
                 weave(nc.vector.tensor_copy, ybf[i][:, PACK * cut :], y32[h][:, :, base + cut : base + hi - lo])
             nc.vector.quantize_mx(out=yw[:, lo:hi].bitcast(FP8X4), scales=ys[:, lo:hi], in_=ybf[i][:])
 
-        ahead = reuse.tile([P, HALF], F32, name="ahead", offset=0, align_bytes=64)
+        ahead = reuse.tile([P, HALF], F32, name="ahead", offset=5120, align_bytes=64)
         pick_input_factors(0, PACK - 1)
         hidden(1)
         hidden(0)
@@ -238,9 +244,7 @@ def tile_picked_bens8_relu_po_kernel(
         store_output(1, 2, PACK)
         for i in range(3):
             output_planes(i)
-            if i == 1:
-                nc.sync.dma_start(out1_v[:, : HALF + CH], yw[:, : HALF + CH])
-        nc.sync.dma_start(out1_v[:, HALF + CH :], yw[:, HALF + CH :])
+            nc.sync.dma_start(out1_v[:, spans[i][0] : spans[i][1]], yw[:, spans[i][0] : spans[i][1]])
         for q in range(4):
             eng = nc.scalar if q % 2 else nc.sync
             eng.dma_start(out_2[0, 4 * q : 4 * q + 4, :].bitcast(I32), ys[32 * q : 32 * q + 4, :].bitcast(I32))

@@ -241,10 +241,13 @@ def tile_picked_bens8_relu_po_kernel(
         for i in (1, 2):
             for t in (2, 3):
                 scale_output(t, *spans[i])
-        store_output(1, 2, PACK)
+            lo, hi = spans[i]
+            nc.sync.dma_start(out0_v[:, 2:, lo:hi], y32[1][:, 2:, lo - HALF : hi - HALF])
         for i in range(3):
             output_planes(i)
-            nc.sync.dma_start(out1_v[:, spans[i][0] : spans[i][1]], yw[:, spans[i][0] : spans[i][1]])
+            if i != 1:
+                words = slice(0, HALF) if i == 0 else slice(HALF, S)
+                nc.sync.dma_start(out1_v[:, words], yw[:, words])
         for q in range(4):
             eng = nc.scalar if q % 2 else nc.sync
             eng.dma_start(out_2[0, 4 * q : 4 * q + 4, :].bitcast(I32), ys[32 * q : 32 * q + 4, :].bitcast(I32))

@@ -67,8 +67,8 @@ def tile_picked_bens8_relu_po_kernel(
         nc.sync.dma_start(rin_sb[0][:], rin_v[0])
         nc.sync.dma_start(mem_sb[:], mem)
         nc.sync.dma_start(offs_sb[:], offs)
-        nc.sync.dma_start(xs_all[0:P:8, :].bitcast(I32), x_scales[0].bitcast(I32))
         nc.sync.dma_start(w1_raw[:, :2, :], w1_v[:, :2, :])
+        nc.sync.dma_start(xs_all[0:P:8, :].bitcast(I32), x_scales[0].bitcast(I32))
         nc.sync.dma_start(rin_sb[1][:], rin_v[1])
         nc.sync.dma_start(w1_raw[:, 2:, :], w1_v[:, 2:, :])
         nc.sync.dma_start(rin_sb[2][:], rin_v[2])

@@ -10,7 +10,7 @@ U16 = mybir.dt.uint16
 U8 = mybir.dt.uint8
 FP8X4 = mybir.dt.float8_e4m3fn_x4
 FP4X4 = mybir.dt.float4_e2m1fn_x4
-RELU = mybir.ActivationFunctionType.Relu
+COPY = mybir.ActivationFunctionType.Copy
 MULT = mybir.AluOpType.mult
 MAX = mybir.AluOpType.max
 
@@ -22,6 +22,7 @@ W = 512
 HALF = 256
 CH = 128
 NCH = S // CH
+W1_VECTOR_SHARE = 84
 
 FLOPS = 2 * 2 * 512 * 512 * 512
 
@@ -33,10 +34,6 @@ def tile_picked_bens8_relu_po_kernel(
     with ExitStack() as ctx:
         keep = ctx.enter_context(tc.tile_pool(name="keep", bufs=1))
         psum = ctx.enter_context(tc.psum_pool(name="psum", bufs=1))
-
-        reuse = ctx.enter_context(tc.tile_pool(name="reuse", bufs=1))
-
-        psum2 = ctx.enter_context(tc.psum_pool(name="psum2", bufs=4))
 
         def tile(name, shape, dtype):
             return keep.tile(shape, dtype, name=name, align_bytes=64)
@@ -51,90 +48,59 @@ def tile_picked_bens8_relu_po_kernel(
         w2w_raw = tile("w2w_raw", [P, 2 * W], U8)
         w2s_raw = tile("w2s_raw", [P, W], U8)
         w2w = tile("w2w", [P, 2 * W], U8)
-        w2s_dealt = tile("w2s_dealt", [P, W], U8)
         w2s = tile("w2s", [P, W], U8)
         rin_sb = [tile(f"rin{t}", [P, W], F32) for t in range(PACK)]
         so_sb = [tile(f"so{t}", [P, W], F32) for t in range(PACK)]
 
         nc.vector.memset(xs_all[:].bitcast(I32), 0)
-        nc.vector.memset(w2s_raw[:].bitcast(I32), 0)
         nc.vector.memset(xs[:].bitcast(I32), 0)
-        nc.vector.memset(w2s[:].bitcast(I32), 0)
+        nc.gpsimd.memset(w2s_raw[:].bitcast(I32), 0)
 
         rin_v = rin.rearrange("(p t) u -> t p u", t=PACK)
         so_v = so.rearrange("(p t) u -> t p u", t=PACK)
-        w1_v = w1.rearrange("(p j) c -> p j c", j=PACK)
-        nc.sync.dma_start(rin_sb[0][:], rin_v[0])
+        nc.sync.dma_start(w1_raw[:], w1.rearrange("(p j) c -> p j c", j=PACK))
         nc.sync.dma_start(mem_sb[:], mem)
         nc.sync.dma_start(offs_sb[:], offs)
-        nc.sync.dma_start(w1_raw[:, :2, :], w1_v[:, :2, :])
         nc.sync.dma_start(xs_all[0:P:8, :].bitcast(I32), x_scales[0].bitcast(I32))
-        nc.sync.dma_start(rin_sb[1][:], rin_v[1])
-        nc.sync.dma_start(w1_raw[:, 2:, :], w1_v[:, 2:, :])
-        nc.sync.dma_start(rin_sb[2][:], rin_v[2])
-        nc.sync.dma_start(w2s_raw[:16, :].bitcast(I32), w2_scales[0].bitcast(I32))
+        for t in range(PACK):
+            nc.sync.dma_start(rin_sb[t][:], rin_v[t])
         nc.sync.dma_start(xw_all[:], x_words[0].rearrange("p c r -> p (c r)").bitcast(I32))
+        for q in range(4):
+            nc.gpsimd.dma_start(
+                w2s_raw[32 * q : 32 * q + 4, :].bitcast(I32), w2_scales[0, 4 * q : 4 * q + 4, :].bitcast(I32)
+            )
 
         nc.vector.tensor_copy(xs_picked[:], xs_all[:].indirect(offs_sb[:]))
         for q in range(4):
             nc.sync.dma_start(
                 xs[32 * q : 32 * q + 4, :].bitcast(I32), xs_picked[32 * q : 32 * q + 32 : 8, :].bitcast(I32)
             )
+        nc.sync.dma_start(so_sb[0][:], so_v[0])
         nc.sync.dma_start(w2w_raw[:].bitcast(I32), w2_words[0].bitcast(I32))
-        nc.sync.dma_start(rin_sb[3][:], rin_v[3])
-        for t in range(PACK):
+        for t in range(1, PACK):
             nc.sync.dma_start(so_sb[t][:], so_v[t])
 
         nc.gpsimd.tensor_copy(
-            w2s_dealt[:].rearrange("p (t m) -> p t m", t=PACK), w2s_raw[:].rearrange("p (m t) -> p t m", t=PACK)
+            w2s[:].rearrange("p (t m) -> p t m", t=PACK), w2s_raw[:].rearrange("p (m t) -> p t m", t=PACK)
         )
         nc.gpsimd.tensor_copy(
             w2w[:].rearrange("p (t m b) -> p t m b", t=PACK, b=2),
             w2w_raw[:].rearrange("p (m t b) -> p t m b", t=PACK, b=2),
         )
-        for q in range(4):
-            nc.sync.dma_start(w2s[32 * q : 32 * q + 4, :].bitcast(I32), w2s_dealt[4 * q : 4 * q + 4, :].bitcast(I32))
-
-        fac = [tile(f"fac{h}", [P, PACK, HALF], F32) for h in range(2)]
-
-        def pick_input_factors(h, t):
-            nc.vector.tensor_copy(fac[h][:, t, :], rin_sb[t][:].indirect(mem_sb[:, 16 * h : 16 * h + 16]))
-
-        for t in range(PACK - 1):
-            for h in range(2):
-                pick_input_factors(h, t)
 
         w1_bf = tile("w1_bf", [P, PACK * W], BF16)
-        w1_dst = w1_bf[:].rearrange("p (t m j) -> p m t j", t=PACK, j=PACK)
-        w1_src = w1_raw[:].rearrange("p j (m t) -> p m t j", t=PACK)
-        for j in (0, 2):
-            nc.scalar.copy(w1_dst[:, :, :, j : j + 2], w1_src[:, :, :, j : j + 2])
+        w1_dst = w1_bf[:].rearrange("p (t m j) -> p m j t", t=PACK, j=PACK)
+        w1_src = w1_raw[:].rearrange("p j (m t) -> p m j t", t=PACK)
+        nc.vector.tensor_copy(w1_dst[:, :W1_VECTOR_SHARE], w1_src[:, :W1_VECTOR_SHARE])
+        nc.scalar.copy(w1_dst[:, W1_VECTOR_SHARE:], w1_src[:, W1_VECTOR_SHARE:])
         w1w = tile("w1w", [P, W], I32)
         w1s = tile("w1s", [P, W], U8)
-        nc.vector.quantize_mx(out=w1w[:].bitcast(FP8X4), scales=w1s[:], in_=w1_bf[:])
 
-        xw = [tile(f"xw{h}", [P, HALF], I32) for h in range(2)]
-        for h in range(2):
-            nc.vector.tensor_copy(
-                xw[h][:].bitcast(U32), xw_all[:].bitcast(U32).indirect(offs_sb[:, 16 * h : 16 * h + 16])
-            )
+        def scalar_gather(dst, window):
+            nc.scalar.activation(dst, window, COPY)
 
-        hid = reuse.tile([P, PACK, CH], F32, name="hid", offset=4096, align_bytes=64)
-        z32 = [tile(f"z32_{c}", [P, PACK, CH], F32) for c in range(NCH)]
-        zbf = [
-            reuse.tile([P, PACK * HALF], BF16, name=f"zbf_{h}", offset=2 * PACK * HALF * h, align_bytes=64)
-            for h in range(2)
-        ]
-        zw = [tile("zw_0", [P, HALF], I32), reuse.tile([P, HALF], I32, name="zw_1", offset=4096, align_bytes=64)]
-        zs = [tile(f"zs_{h}", [P, HALF], U8) for h in range(2)]
-        o32 = [tile(f"o32_{h}", [P, PACK, HALF], F32) for h in range(2)]
-        y32 = [tile(f"y32_{h}", [P, PACK, HALF], F32) for h in range(2)]
-        spans = [(0, HALF), (HALF, HALF + CH), (HALF + CH, S)]
-        ybf = [tile(f"ybf_{i}", [P, PACK * (hi - lo)], BF16) for i, (lo, hi) in enumerate(spans)]
-        yw = tile("yw", [P, S], I32)
-        ys = tile("ys", [P, S], U8)
-        out0_v = out_0.rearrange("(p t) n -> p t n", t=PACK)
-        out1_v = out_1[0].rearrange("p c r -> p (c r)").bitcast(I32)
+        def pick(gather, dst, table, lo, hi):
+            gather(dst, table[:].indirect(mem_sb[:, lo // 16 : hi // 16]))
 
         def woven(ap):
             return ap.rearrange("p (c i t) -> p c t i", i=4, t=PACK)
@@ -145,109 +111,112 @@ def tile_picked_bens8_relu_po_kernel(
         def weave(copy, dst, src):
             copy(woven(dst), by_planes(src))
 
-        def first_product(c, planes, pool, name):
+        rin_picked = [tile(f"rin_picked{h}", [P, PACK, HALF], F32) for h in range(2)]
+        rin_woven = [tile(f"rin_woven{c}", [P, PACK * CH], F32) for c in range(NCH)]
+        so_picked = [tile(f"so_picked{h}", [P, PACK, HALF], F32) for h in range(2)]
+
+        for h in range(2):
+            pick(scalar_gather, rin_picked[h][:, 0, :], rin_sb[0], h * HALF, (h + 1) * HALF)
+        nc.vector.quantize_mx(out=w1w[:].bitcast(FP8X4), scales=w1s[:], in_=w1_bf[:])
+        for h in range(2):
+            pick(nc.vector.tensor_copy, rin_picked[h][:, 1, :], rin_sb[1], h * HALF, (h + 1) * HALF)
+        for h in range(2):
+            pick(scalar_gather, rin_picked[h][:, 2, :], rin_sb[2], h * HALF, (h + 1) * HALF)
+        pick(nc.vector.tensor_copy, rin_picked[0][:, 3, :], rin_sb[3], 0, HALF)
+        pick(scalar_gather, rin_picked[1][:, 3, :], rin_sb[3], HALF, S)
+        for c in range(NCH):
             h, base = divmod(c * CH, HALF)
-            acc = pool.tile([P, len(planes), CH], F32, name=name)
-            for i, t in enumerate(planes):
+            copy = nc.vector.tensor_copy if h == 0 else nc.scalar.copy
+            weave(copy, rin_woven[c][:], rin_picked[h][:, :, base : base + CH])
+
+        word_spans = [(0, CH), (CH, HALF), (HALF, S)]
+        xw = [tile(f"xw{i}", [P, hi - lo], I32) for i, (lo, hi) in enumerate(word_spans)]
+        for i, (lo, hi) in enumerate(word_spans):
+            nc.vector.tensor_copy(
+                xw[i][:].bitcast(U32), xw_all[:].bitcast(U32).indirect(offs_sb[:, lo // 16 : hi // 16])
+            )
+        for h in range(2):
+            for t in range(PACK):
+                pick(scalar_gather, so_picked[h][:, t, :], so_sb[t], h * HALF, (h + 1) * HALF)
+
+        zbf = [tile(f"zbf_{h}", [P, PACK * HALF], BF16) for h in range(2)]
+        zw = [tile(f"zw_{h}", [P, HALF], I32) for h in range(2)]
+        zs = [tile(f"zs_{h}", [P, HALF], U8) for h in range(2)]
+        y32 = [tile(f"y32_{c}", [P, PACK, CH], F32) for c in range(NCH)]
+        spans = [(0, HALF), (HALF, HALF + CH), (HALF + CH, S)]
+        ybf = [tile(f"ybf_{i}", [P, PACK * (hi - lo)], BF16) for i, (lo, hi) in enumerate(spans)]
+        yw = tile("yw", [P, S], I32)
+        ys = tile("ys", [P, S], U8)
+        out0_v = out_0.rearrange("(p t) n -> p t n", t=PACK)
+        out1_v = out_1[0].rearrange("p c r -> p (c r)").bitcast(I32)
+
+        def hidden(c):
+            h, base = divmod(c * CH, HALF)
+            words = xw[min(c, 2)][:, (c == 3) * CH : (c == 3) * CH + CH]
+            acc = psum.tile([P, PACK, CH], F32, name=f"acc1_{c}")
+            for t in range(PACK):
                 nc.tensor.matmul_mx(
-                    out=acc[:, i, :],
+                    out=acc[:, t, :],
                     lhsT=w1w[:, P * t : P * (t + 1)].bitcast(FP8X4),
                     lhsT_scale=w1s[:, P * t : P * (t + 1)],
-                    rhs=xw[h][:, base : base + CH].bitcast(FP8X4),
+                    rhs=words.bitcast(FP8X4),
                     rhs_scale=xs[:, c * CH : (c + 1) * CH],
                     start=True,
                     stop=True,
                 )
-            return acc
-
-        def hidden(c):
-            h, base = divmod(c * CH, HALF)
-            factors = fac[h][:, :, base : base + CH]
-            if c == 1:
-                for lo in (0, 2):
-                    nc.scalar.activation(hid[:, lo : lo + 2, :], first_product(c, [lo, lo + 1], psum2, "acc2")[:], RELU)
-                nc.gpsimd.tensor_tensor(
-                    woven(zbf[h][:, PACK * base : PACK * (base + CH)]), by_planes(hid[:]), by_planes(factors), MULT
-                )
-            else:
-                acc = first_product(c, range(PACK), psum, f"acc1_{c}")
-                nc.vector.scalar_tensor_tensor(z32[c][:], acc[:], 0.0, factors, MAX, MULT)
-
-        def round_hidden(c):
-            h, base = divmod(c * CH, HALF)
-            weave(nc.scalar.copy, zbf[h][:, PACK * base : PACK * (base + CH)], z32[c][:])
+            nc.vector.scalar_tensor_tensor(
+                zbf[h][:, PACK * base : PACK * (base + CH)].rearrange("p (c t) -> p c t", t=PACK),
+                acc[:].rearrange("p t c -> p c t"),
+                0.0,
+                rin_woven[c][:].rearrange("p (c t) -> p c t", t=PACK),
+                MAX,
+                MULT,
+            )
 
         def quantize_hidden(h):
             nc.vector.quantize_mx(out=zw[h][:].bitcast(FP8X4), scales=zs[h][:], in_=zbf[h][:])
 
-        def second_product(h, planes):
-            acc = psum2.tile([P, len(planes), HALF], F32, name="acc2")
-            for i, t in enumerate(planes):
+        def output(c):
+            h, base = divmod(c * CH, HALF)
+            acc = psum.tile([P, PACK, CH], F32, name=f"acc2_{c}")
+            for t in range(PACK):
                 nc.tensor.matmul_mx(
-                    out=acc[:, i, :],
+                    out=acc[:, t, :],
                     lhsT=w2w[:, 2 * P * t : 2 * P * (t + 1)].bitcast(FP4X4),
                     lhsT_scale=w2s[:, P * t : P * (t + 1)],
-                    rhs=zw[h][:].bitcast(FP8X4),
-                    rhs_scale=zs[h][:],
+                    rhs=zw[h][:, base : base + CH].bitcast(FP8X4),
+                    rhs_scale=zs[h][:, base : base + CH],
                     start=True,
                     stop=True,
                 )
-            return acc
+            nc.vector.tensor_tensor(y32[c][:], acc[:], so_picked[h][:, :, base : base + CH], MULT)
+            nc.sync.dma_start(out0_v[:, :, c * CH : (c + 1) * CH], y32[c][:])
 
-        def scale_output(t, lo, hi):
-            h, base = divmod(lo, HALF)
-            cols = slice(base, base + hi - lo)
-            nc.vector.tensor_tensor(
-                y32[h][:, t, cols], so_sb[t][:].indirect(mem_sb[:, lo // 16 : hi // 16]), o32[h][:, t, cols], MULT
-            )
+        def round_output(c, copy):
+            i = max(c - 1, 0)
+            base = c * CH - spans[i][0]
+            weave(copy, ybf[i][:, PACK * base : PACK * (base + CH)], y32[c][:])
 
-        def store_output(h, lo, hi):
-            nc.sync.dma_start(out0_v[:, lo:hi, h * HALF : (h + 1) * HALF], y32[h][:, lo:hi, :])
-
-        def output_planes(i):
+        def quantize_output(i):
             lo, hi = spans[i]
-            h, base = divmod(lo, HALF)
-            cut = 48 if i == len(spans) - 1 else hi - lo
-            weave(nc.scalar.copy, ybf[i][:, : PACK * cut], y32[h][:, :, base : base + cut])
-            if cut < hi - lo:
-                weave(nc.vector.tensor_copy, ybf[i][:, PACK * cut :], y32[h][:, :, base + cut : base + hi - lo])
             nc.vector.quantize_mx(out=yw[:, lo:hi].bitcast(FP8X4), scales=ys[:, lo:hi], in_=ybf[i][:])
 
-        ahead = reuse.tile([P, HALF], F32, name="ahead", offset=5120, align_bytes=64)
-        pick_input_factors(0, PACK - 1)
-        hidden(1)
-        hidden(0)
-        round_hidden(0)
-        pick_input_factors(1, PACK - 1)
-        for c in (2, 3):
+        for c in range(3):
             hidden(c)
         quantize_hidden(0)
-        nc.vector.tensor_copy(ahead[:], so_sb[0][:].indirect(mem_sb[:, :16]))
-        for c in (2, 3):
-            round_hidden(c)
-        nc.scalar.copy(o32[0][:, 1, :], second_product(0, [1])[:, 0, :])
-        first = second_product(0, [0])
-        nc.scalar.copy(o32[0][:, 2:, :], second_product(0, [2, 3])[:])
+        hidden(3)
+        output(0)
         quantize_hidden(1)
-        nc.vector.tensor_tensor(y32[0][:, 0, :], first[:, 0, :], ahead[:], MULT)
-        for t in range(1, PACK):
-            scale_output(t, 0, HALF)
-        store_output(0, 0, PACK)
-        for pair in range(2):
-            nc.scalar.copy(o32[1][:, 2 * pair : 2 * pair + 2, :], second_product(1, [2 * pair, 2 * pair + 1])[:])
-        for t in range(2):
-            scale_output(t, HALF, S)
-        store_output(1, 0, 2)
-        for i in (1, 2):
-            for t in (2, 3):
-                scale_output(t, *spans[i])
-            lo, hi = spans[i]
-            nc.sync.dma_start(out0_v[:, 2:, lo:hi], y32[1][:, 2:, lo - HALF : hi - HALF])
-        for i in range(3):
-            output_planes(i)
-            if i != 1:
-                words = slice(0, HALF) if i == 0 else slice(HALF, S)
-                nc.sync.dma_start(out1_v[:, words], yw[:, words])
+        for c in range(1, NCH):
+            output(c)
+        for c in range(3):
+            round_output(c, nc.scalar.copy)
+        quantize_output(0)
+        nc.sync.dma_start(out1_v[:, :HALF], yw[:, :HALF])
+        round_output(3, nc.vector.tensor_copy)
+        quantize_output(1)
+        quantize_output(2)
+        nc.sync.dma_start(out1_v[:, HALF:], yw[:, HALF:])
         for q in range(4):
             eng = nc.scalar if q % 2 else nc.sync
             eng.dma_start(out_2[0, 4 * q : 4 * q + 4, :].bitcast(I32), ys[32 * q : 32 * q + 4, :].bitcast(I32))

@@ -12,6 +12,7 @@ FP8X4 = mybir.dt.float8_e4m3fn_x4
 FP4X4 = mybir.dt.float4_e2m1fn_x4
 COPY = mybir.ActivationFunctionType.Copy
 MULT = mybir.AluOpType.mult
+ADD = mybir.AluOpType.add
 MAX = mybir.AluOpType.max
 
 P = 128
@@ -22,7 +23,8 @@ W = 512
 HALF = 256
 CH = 128
 NCH = S // CH
-W1_VECTOR_SHARE = 84
+ROW = 4 * W
+W1_VECTOR_SHARE = 96
 
 FLOPS = 2 * 2 * 512 * 512 * 512
 
@@ -33,6 +35,7 @@ def tile_picked_bens8_relu_po_kernel(
     nc = tc.nc
     with ExitStack() as ctx:
         keep = ctx.enter_context(tc.tile_pool(name="keep", bufs=1))
+        reuse = ctx.enter_context(tc.tile_pool(name="reuse", bufs=1))
         psum = ctx.enter_context(tc.psum_pool(name="psum", bufs=1))
 
         def tile(name, shape, dtype):
@@ -44,13 +47,19 @@ def tile_picked_bens8_relu_po_kernel(
         xs_all = tile("xs_all", [P, T], U8)
         xs_picked = tile("xs_picked", [P, S], U8)
         xs = tile("xs", [P, S], U8)
-        w1_raw = tile("w1_raw", [P, PACK, W], F32)
-        w2w_raw = tile("w2w_raw", [P, 2 * W], U8)
+        w1_raw = reuse.tile([P, PACK, W], F32, name="w1_raw", offset=0, align_bytes=64)
+        w2w_raw = reuse.tile([P, 2 * (W - CH)], U8, name="w2w_raw", offset=3 * ROW, align_bytes=64)
         w2s_raw = tile("w2s_raw", [P, W], U8)
+        w2w_early = tile("w2w_early", [P, 2 * CH], U8)
         w2w = tile("w2w", [P, 2 * W], U8)
         w2s = tile("w2s", [P, W], U8)
-        rin_sb = [tile(f"rin{t}", [P, W], F32) for t in range(PACK)]
-        so_sb = [tile(f"so{t}", [P, W], F32) for t in range(PACK)]
+        rin_sb = [
+            reuse.tile([P, W], F32, name=f"rin{t}", offset=(PACK + t) * ROW, align_bytes=64) for t in range(PACK)
+        ]
+        so_sb = [
+            reuse.tile([P, W], F32, name=f"so{t}", offset=row * ROW, align_bytes=64)
+            for t, row in enumerate((PACK + 2, PACK + 3, 1, 2))
+        ]
 
         nc.vector.memset(xs_all[:].bitcast(I32), 0)
         nc.vector.memset(xs[:].bitcast(I32), 0)
@@ -58,12 +67,16 @@ def tile_picked_bens8_relu_po_kernel(
 
         rin_v = rin.rearrange("(p t) u -> t p u", t=PACK)
         so_v = so.rearrange("(p t) u -> t p u", t=PACK)
-        nc.sync.dma_start(w1_raw[:], w1.rearrange("(p j) c -> p j c", j=PACK))
+        w2_v = w2_words[0].bitcast(I32)
+        nc.sync.dma_start(w2w_early[:].bitcast(I32), w2_v[:, : CH // 2])
         nc.sync.dma_start(mem_sb[:], mem)
+        nc.sync.dma_start(rin_sb[0][:], rin_v[0])
+        nc.sync.dma_start(rin_sb[1][:], rin_v[1])
         nc.sync.dma_start(offs_sb[:], offs)
         nc.sync.dma_start(xs_all[0:P:8, :].bitcast(I32), x_scales[0].bitcast(I32))
-        for t in range(PACK):
+        for t in range(2, PACK):
             nc.sync.dma_start(rin_sb[t][:], rin_v[t])
+        nc.sync.dma_start(w1_raw[:], w1.rearrange("(p j) c -> p j c", j=PACK))
         nc.sync.dma_start(xw_all[:], x_words[0].rearrange("p c r -> p (c r)").bitcast(I32))
         for q in range(4):
             nc.gpsimd.dma_start(
@@ -75,24 +88,18 @@ def tile_picked_bens8_relu_po_kernel(
             nc.sync.dma_start(
                 xs[32 * q : 32 * q + 4, :].bitcast(I32), xs_picked[32 * q : 32 * q + 32 : 8, :].bitcast(I32)
             )
-        nc.sync.dma_start(so_sb[0][:], so_v[0])
-        nc.sync.dma_start(w2w_raw[:].bitcast(I32), w2_words[0].bitcast(I32))
-        for t in range(1, PACK):
-            nc.sync.dma_start(so_sb[t][:], so_v[t])
 
         nc.gpsimd.tensor_copy(
             w2s[:].rearrange("p (t m) -> p t m", t=PACK), w2s_raw[:].rearrange("p (m t) -> p t m", t=PACK)
         )
-        nc.gpsimd.tensor_copy(
-            w2w[:].rearrange("p (t m b) -> p t m b", t=PACK, b=2),
-            w2w_raw[:].rearrange("p (m t b) -> p t m b", t=PACK, b=2),
+        nc.scalar.copy(
+            w2w[:].bitcast(U16).rearrange("p (t m) -> p t m", t=PACK)[:, :, : CH // PACK],
+            w2w_early[:].bitcast(U16).rearrange("p (m t) -> p t m", t=PACK),
         )
 
         w1_bf = tile("w1_bf", [P, PACK * W], BF16)
         w1_dst = w1_bf[:].rearrange("p (t m j) -> p m j t", t=PACK, j=PACK)
         w1_src = w1_raw[:].rearrange("p j (m t) -> p m j t", t=PACK)
-        nc.vector.tensor_copy(w1_dst[:, :W1_VECTOR_SHARE], w1_src[:, :W1_VECTOR_SHARE])
-        nc.scalar.copy(w1_dst[:, W1_VECTOR_SHARE:], w1_src[:, W1_VECTOR_SHARE:])
         w1w = tile("w1w", [P, W], I32)
         w1s = tile("w1s", [P, W], U8)
 
@@ -112,22 +119,38 @@ def tile_picked_bens8_relu_po_kernel(
             copy(woven(dst), by_planes(src))
 
         rin_picked = [tile(f"rin_picked{h}", [P, PACK, HALF], F32) for h in range(2)]
-        rin_woven = [tile(f"rin_woven{c}", [P, PACK * CH], F32) for c in range(NCH)]
+        rin_woven = [tile(f"rin_woven{c}", [P, PACK * CH], F32) for c in range(NCH - 1)]
+        rin_woven.append(reuse.tile([P, PACK * CH], F32, name="rin_woven_last", offset=0, align_bytes=64))
         so_picked = [tile(f"so_picked{h}", [P, PACK, HALF], F32) for h in range(2)]
 
         for h in range(2):
-            pick(scalar_gather, rin_picked[h][:, 0, :], rin_sb[0], h * HALF, (h + 1) * HALF)
-        nc.vector.quantize_mx(out=w1w[:].bitcast(FP8X4), scales=w1s[:], in_=w1_bf[:])
+            pick(nc.vector.tensor_copy, rin_picked[h][:, 0, :], rin_sb[0], h * HALF, (h + 1) * HALF)
         for h in range(2):
-            pick(nc.vector.tensor_copy, rin_picked[h][:, 1, :], rin_sb[1], h * HALF, (h + 1) * HALF)
+            pick(scalar_gather, rin_picked[h][:, 1, :], rin_sb[1], h * HALF, (h + 1) * HALF)
         for h in range(2):
             pick(scalar_gather, rin_picked[h][:, 2, :], rin_sb[2], h * HALF, (h + 1) * HALF)
         pick(nc.vector.tensor_copy, rin_picked[0][:, 3, :], rin_sb[3], 0, HALF)
         pick(scalar_gather, rin_picked[1][:, 3, :], rin_sb[3], HALF, S)
-        for c in range(NCH):
+
+        def weave_factors(c):
             h, base = divmod(c * CH, HALF)
-            copy = nc.vector.tensor_copy if h == 0 else nc.scalar.copy
+            copy = nc.vector.tensor_copy if c < NCH - 1 else nc.scalar.copy
             weave(copy, rin_woven[c][:], rin_picked[h][:, :, base : base + CH])
+
+        for c in range(NCH - 1):
+            weave_factors(c)
+        nc.vector.tensor_copy(w1_dst[:, :W1_VECTOR_SHARE], w1_src[:, :W1_VECTOR_SHARE])
+        nc.scalar.copy(w1_dst[:, W1_VECTOR_SHARE:], w1_src[:, W1_VECTOR_SHARE:])
+        nc.vector.quantize_mx(out=w1w[:].bitcast(FP8X4), scales=w1s[:], in_=w1_bf[:])
+        weave_factors(NCH - 1)
+        for t in range(PACK):
+            nc.sync.dma_start(so_sb[t][:], so_v[t])
+            if t == 1:
+                nc.sync.dma_start(w2w_raw[:].bitcast(I32), w2_v[:, CH // 2 :])
+        nc.gpsimd.tensor_copy(
+            w2w[:].rearrange("p (t m b) -> p t m b", t=PACK, b=2)[:, :, CH // PACK :, :],
+            w2w_raw[:].rearrange("p (m t b) -> p t m b", t=PACK, b=2),
+        )
 
         word_spans = [(0, CH), (CH, HALF), (HALF, S)]
         xw = [tile(f"xw{i}", [P, hi - lo], I32) for i, (lo, hi) in enumerate(word_spans)]
@@ -135,15 +158,20 @@ def tile_picked_bens8_relu_po_kernel(
             nc.vector.tensor_copy(
                 xw[i][:].bitcast(U32), xw_all[:].bitcast(U32).indirect(offs_sb[:, lo // 16 : hi // 16])
             )
-        for h in range(2):
-            for t in range(PACK):
-                pick(scalar_gather, so_picked[h][:, t, :], so_sb[t], h * HALF, (h + 1) * HALF)
+        for pair in range(2):
+            for h in range(2):
+                for t in (2 * pair, 2 * pair + 1):
+                    pick(scalar_gather, so_picked[h][:, t, :], so_sb[t], h * HALF, (h + 1) * HALF)
 
-        zbf = [tile(f"zbf_{h}", [P, PACK * HALF], BF16) for h in range(2)]
-        zw = [tile(f"zw_{h}", [P, HALF], I32) for h in range(2)]
-        zs = [tile(f"zs_{h}", [P, HALF], U8) for h in range(2)]
-        y32 = [tile(f"y32_{c}", [P, PACK, CH], F32) for c in range(NCH)]
         spans = [(0, HALF), (HALF, HALF + CH), (HALF + CH, S)]
+        zbf = [tile(f"zbf_{i}", [P, PACK * (hi - lo)], BF16) for i, (lo, hi) in enumerate(spans)]
+        zw = [tile(f"zw_{i}", [P, hi - lo], I32) for i, (lo, hi) in enumerate(spans)]
+        zs = [tile(f"zs_{i}", [P, hi - lo], U8) for i, (lo, hi) in enumerate(spans)]
+        y32 = [tile(f"y32_{i}", [P, PACK, hi - lo], F32) for i, (lo, hi) in enumerate(spans)]
+
+        def span_of(c):
+            i = max(c - 1, 0)
+            return i, c * CH - spans[i][0]
         ybf = [tile(f"ybf_{i}", [P, PACK * (hi - lo)], BF16) for i, (lo, hi) in enumerate(spans)]
         yw = tile("yw", [P, S], I32)
         ys = tile("ys", [P, S], U8)
@@ -151,7 +179,7 @@ def tile_picked_bens8_relu_po_kernel(
         out1_v = out_1[0].rearrange("p c r -> p (c r)").bitcast(I32)
 
         def hidden(c):
-            h, base = divmod(c * CH, HALF)
+            h, base = span_of(c)
             words = xw[min(c, 2)][:, (c == 3) * CH : (c == 3) * CH + CH]
             acc = psum.tile([P, PACK, CH], F32, name=f"acc1_{c}")
             for t in range(PACK):
@@ -176,26 +204,27 @@ def tile_picked_bens8_relu_po_kernel(
         def quantize_hidden(h):
             nc.vector.quantize_mx(out=zw[h][:].bitcast(FP8X4), scales=zs[h][:], in_=zbf[h][:])
 
-        def output(c):
-            h, base = divmod(c * CH, HALF)
-            acc = psum.tile([P, PACK, CH], F32, name=f"acc2_{c}")
-            for t in range(PACK):
+        def output(i, planes):
+            lo, hi = spans[i]
+            h, base = divmod(lo, HALF)
+            acc = psum.tile([P, len(planes), hi - lo], F32, name=f"acc2_{i}_{planes[0]}")
+            for n, t in enumerate(planes):
                 nc.tensor.matmul_mx(
-                    out=acc[:, t, :],
+                    out=acc[:, n, :],
                     lhsT=w2w[:, 2 * P * t : 2 * P * (t + 1)].bitcast(FP4X4),
                     lhsT_scale=w2s[:, P * t : P * (t + 1)],
-                    rhs=zw[h][:, base : base + CH].bitcast(FP8X4),
-                    rhs_scale=zs[h][:, base : base + CH],
+                    rhs=zw[i][:].bitcast(FP8X4),
+                    rhs_scale=zs[i][:],
                     start=True,
                     stop=True,
                 )
-            nc.vector.tensor_tensor(y32[c][:], acc[:], so_picked[h][:, :, base : base + CH], MULT)
-            nc.sync.dma_start(out0_v[:, :, c * CH : (c + 1) * CH], y32[c][:])
+            rows = slice(planes[0], planes[-1] + 1)
+            nc.vector.tensor_tensor(y32[i][:, rows, :], acc[:], so_picked[h][:, rows, base : base + hi - lo], MULT)
+            nc.sync.dma_start(out0_v[:, rows, lo:hi], y32[i][:, rows, :])
 
         def round_output(c, copy):
-            i = max(c - 1, 0)
-            base = c * CH - spans[i][0]
-            weave(copy, ybf[i][:, PACK * base : PACK * (base + CH)], y32[c][:])
+            i, at = span_of(c)
+            weave(copy, ybf[i][:, PACK * at : PACK * (at + CH)], y32[i][:, :, at : at + CH])
 
         def quantize_output(i):
             lo, hi = spans[i]
@@ -205,11 +234,21 @@ def tile_picked_bens8_relu_po_kernel(
             hidden(c)
         quantize_hidden(0)
         hidden(3)
-        output(0)
         quantize_hidden(1)
-        for c in range(1, NCH):
-            output(c)
-        for c in range(3):
+        output(0, [0, 1])
+        quantize_hidden(2)
+        output(0, [2, 3])
+        for i in (1, 2):
+            output(i, range(PACK))
+        nc.gpsimd.tensor_scalar(
+            ybf[0][:, : PACK * CH].rearrange("p (c t) -> p c t", t=PACK),
+            y32[0][:, :, :CH].rearrange("p t c -> p c t"),
+            1.0,
+            -0.0,
+            MULT,
+            ADD,
+        )
+        for c in (1, 2):
             round_output(c, nc.scalar.copy)
         quantize_output(0)
         nc.sync.dma_start(out1_v[:, :HALF], yw[:, :HALF])

@@ -48,11 +48,11 @@ def tile_picked_bens8_relu_po_kernel(
         xs_picked = tile("xs_picked", [P, S], U8)
         xs = tile("xs", [P, S], U8)
         w1_raw = reuse.tile([P, PACK, W], F32, name="w1_raw", offset=0, align_bytes=64)
-        w2w_raw = reuse.tile([P, 2 * (W - CH)], U8, name="w2w_raw", offset=3 * ROW, align_bytes=64)
+        w2w_raw = reuse.tile([P, 2 * (W - CH)], U8, name="w2w_raw", offset=(PACK + 1) * ROW, align_bytes=64)
         w2s_raw = tile("w2s_raw", [P, W], U8)
         w2w_early = tile("w2w_early", [P, 2 * CH], U8)
         w2w = tile("w2w", [P, 2 * W], U8)
-        w2s = tile("w2s", [P, W], U8)
+        w2s = reuse.tile([P, W], U8, name="w2s", offset=2 * PACK * ROW, align_bytes=64)
         rin_sb = [
             reuse.tile([P, W], F32, name=f"rin{t}", offset=(PACK + t) * ROW, align_bytes=64) for t in range(PACK)
         ]
@@ -89,15 +89,12 @@ def tile_picked_bens8_relu_po_kernel(
                 xs[32 * q : 32 * q + 4, :].bitcast(I32), xs_picked[32 * q : 32 * q + 32 : 8, :].bitcast(I32)
             )
 
-        nc.gpsimd.tensor_copy(
-            w2s[:].rearrange("p (t m) -> p t m", t=PACK), w2s_raw[:].rearrange("p (m t) -> p t m", t=PACK)
-        )
         nc.scalar.copy(
             w2w[:].bitcast(U16).rearrange("p (t m) -> p t m", t=PACK)[:, :, : CH // PACK],
             w2w_early[:].bitcast(U16).rearrange("p (m t) -> p t m", t=PACK),
         )
 
-        w1_bf = tile("w1_bf", [P, PACK * W], BF16)
+        w1_bf = reuse.tile([P, PACK * W], BF16, name="w1_bf", offset=2 * PACK * ROW, align_bytes=64)
         w1_dst = w1_bf[:].rearrange("p (t m j) -> p m j t", t=PACK, j=PACK)
         w1_src = w1_raw[:].rearrange("p j (m t) -> p m j t", t=PACK)
         w1w = tile("w1w", [P, W], I32)
@@ -143,13 +140,15 @@ def tile_picked_bens8_relu_po_kernel(
         nc.scalar.copy(w1_dst[:, W1_VECTOR_SHARE:], w1_src[:, W1_VECTOR_SHARE:])
         nc.vector.quantize_mx(out=w1w[:].bitcast(FP8X4), scales=w1s[:], in_=w1_bf[:])
         weave_factors(NCH - 1)
+        nc.gpsimd.tensor_copy(
+            w2s[:].rearrange("p (t m) -> p t m", t=PACK), w2s_raw[:].rearrange("p (m t) -> p t m", t=PACK)
+        )
+        nc.sync.dma_start(w2w_raw[:].bitcast(I32), w2_v[:, CH // 2 :])
         for t in range(PACK):
             nc.sync.dma_start(so_sb[t][:], so_v[t])
-            if t == 1:
-                nc.sync.dma_start(w2w_raw[:].bitcast(I32), w2_v[:, CH // 2 :])
-        nc.gpsimd.tensor_copy(
-            w2w[:].rearrange("p (t m b) -> p t m b", t=PACK, b=2)[:, :, CH // PACK :, :],
-            w2w_raw[:].rearrange("p (m t b) -> p t m b", t=PACK, b=2),
+        nc.scalar.copy(
+            w2w[:].bitcast(U16).rearrange("p (t m) -> p t m", t=PACK)[:, :, CH // PACK :],
+            w2w_raw[:].bitcast(U16).rearrange("p (m t) -> p t m", t=PACK),
         )
 
         word_spans = [(0, CH), (CH, HALF), (HALF, S)]

@@ -24,7 +24,10 @@ HALF = 256
 CH = 128
 NCH = S // CH
 ROW = 4 * W
-W1_VECTOR_SHARE = 96
+RIN_AT = [4 * ROW, 5 * ROW, 6 * ROW, 9 * ROW]
+SO_AT = [5 * ROW + 256, 7 * ROW - 256, 8 * ROW + ROW // 2, 9 * ROW + ROW // 2]
+W1_VECTOR_SHARE = 80
+EARLY = 192
 
 FLOPS = 2 * 2 * 512 * 512 * 512
 
@@ -48,27 +51,25 @@ def tile_picked_bens8_relu_po_kernel(
         xs_picked = tile("xs_picked", [P, S], U8)
         xs = tile("xs", [P, S], U8)
         w1_raw = reuse.tile([P, PACK, W], F32, name="w1_raw", offset=0, align_bytes=64)
-        w2w_raw = reuse.tile([P, 2 * (W - CH)], U8, name="w2w_raw", offset=(PACK + 1) * ROW, align_bytes=64)
+        w2w_raw = reuse.tile([P, 2 * (W - EARLY)], U8, name="w2w_raw", offset=RIN_AT[2] + 256, align_bytes=64)
         w2s_raw = tile("w2s_raw", [P, W], U8)
-        w2w_early = tile("w2w_early", [P, 2 * CH], U8)
+        w2w_early = tile("w2w_early", [P, 2 * EARLY], U8)
         w2w = tile("w2w", [P, 2 * W], U8)
-        w2s = reuse.tile([P, W], U8, name="w2s", offset=2 * PACK * ROW, align_bytes=64)
+        w2s = tile("w2s", [P, W], U8)
         rin_sb = [
-            reuse.tile([P, W], F32, name=f"rin{t}", offset=(PACK + t) * ROW, align_bytes=64) for t in range(PACK)
+            reuse.tile([P, W], F32, name=f"rin{t}", offset=RIN_AT[t], align_bytes=64) for t in range(PACK)
         ]
         so_sb = [
-            reuse.tile([P, W], F32, name=f"so{t}", offset=row * ROW, align_bytes=64)
-            for t, row in enumerate((PACK + 2, PACK + 3, 1, 2))
+            reuse.tile([P, W], F32, name=f"so{t}", offset=SO_AT[t], align_bytes=64) for t in range(PACK)
         ]
 
         nc.vector.memset(xs_all[:].bitcast(I32), 0)
-        nc.vector.memset(xs[:].bitcast(I32), 0)
         nc.gpsimd.memset(w2s_raw[:].bitcast(I32), 0)
 
         rin_v = rin.rearrange("(p t) u -> t p u", t=PACK)
         so_v = so.rearrange("(p t) u -> t p u", t=PACK)
         w2_v = w2_words[0].bitcast(I32)
-        nc.sync.dma_start(w2w_early[:].bitcast(I32), w2_v[:, : CH // 2])
+        nc.sync.dma_start(w2w_early[:].bitcast(I32), w2_v[:, : EARLY // 2])
         nc.sync.dma_start(mem_sb[:], mem)
         nc.sync.dma_start(rin_sb[0][:], rin_v[0])
         nc.sync.dma_start(rin_sb[1][:], rin_v[1])
@@ -84,17 +85,16 @@ def tile_picked_bens8_relu_po_kernel(
             )
 
         nc.vector.tensor_copy(xs_picked[:], xs_all[:].indirect(offs_sb[:]))
-        for q in range(4):
-            nc.sync.dma_start(
-                xs[32 * q : 32 * q + 4, :].bitcast(I32), xs_picked[32 * q : 32 * q + 32 : 8, :].bitcast(I32)
-            )
+        nc.vector.tensor_copy(xs[:].bitcast(I32), xs_picked[:].bitcast(I32))
+        for r in range(1, 4):
+            nc.sync.dma_start(xs[r:P:32, :].bitcast(I32), xs_picked[8 * r : P : 32, :].bitcast(I32))
 
         nc.scalar.copy(
-            w2w[:].bitcast(U16).rearrange("p (t m) -> p t m", t=PACK)[:, :, : CH // PACK],
+            w2w[:].bitcast(U16).rearrange("p (t m) -> p t m", t=PACK)[:, :, : EARLY // PACK],
             w2w_early[:].bitcast(U16).rearrange("p (m t) -> p t m", t=PACK),
         )
 
-        w1_bf = reuse.tile([P, PACK * W], BF16, name="w1_bf", offset=2 * PACK * ROW, align_bytes=64)
+        w1_bf = tile("w1_bf", [P, PACK * W], BF16)
         w1_dst = w1_bf[:].rearrange("p (t m j) -> p m j t", t=PACK, j=PACK)
         w1_src = w1_raw[:].rearrange("p j (m t) -> p m j t", t=PACK)
         w1w = tile("w1w", [P, W], I32)
@@ -116,9 +116,15 @@ def tile_picked_bens8_relu_po_kernel(
             copy(woven(dst), by_planes(src))
 
         rin_picked = [tile(f"rin_picked{h}", [P, PACK, HALF], F32) for h in range(2)]
-        rin_woven = [tile(f"rin_woven{c}", [P, PACK * CH], F32) for c in range(NCH - 1)]
-        rin_woven.append(reuse.tile([P, PACK * CH], F32, name="rin_woven_last", offset=0, align_bytes=64))
-        so_picked = [tile(f"so_picked{h}", [P, PACK, HALF], F32) for h in range(2)]
+        rin_woven = [tile(f"rin_woven{c}", [P, PACK * CH], F32) for c in range(2)]
+        rin_woven.extend(
+            reuse.tile([P, PACK * CH], F32, name=f"rin_woven{c}", offset=c * ROW, align_bytes=64) for c in (2, 3)
+        )
+        so_first = tile("so_first", [P, PACK, HALF], F32)
+        so_second = [
+            reuse.tile([P, 2, HALF], F32, name="so_second0", offset=SO_AT[3], align_bytes=64),
+            tile("so_second1", [P, 2, HALF], F32),
+        ]
 
         for h in range(2):
             pick(nc.vector.tensor_copy, rin_picked[h][:, 0, :], rin_sb[0], h * HALF, (h + 1) * HALF)
@@ -134,21 +140,22 @@ def tile_picked_bens8_relu_po_kernel(
             copy = nc.vector.tensor_copy if c < NCH - 1 else nc.scalar.copy
             weave(copy, rin_woven[c][:], rin_picked[h][:, :, base : base + CH])
 
-        for c in range(NCH - 1):
+        for c in range(2):
             weave_factors(c)
         nc.vector.tensor_copy(w1_dst[:, :W1_VECTOR_SHARE], w1_src[:, :W1_VECTOR_SHARE])
         nc.scalar.copy(w1_dst[:, W1_VECTOR_SHARE:], w1_src[:, W1_VECTOR_SHARE:])
+        weave_factors(2)
         nc.vector.quantize_mx(out=w1w[:].bitcast(FP8X4), scales=w1s[:], in_=w1_bf[:])
         weave_factors(NCH - 1)
         nc.gpsimd.tensor_copy(
             w2s[:].rearrange("p (t m) -> p t m", t=PACK), w2s_raw[:].rearrange("p (m t) -> p t m", t=PACK)
         )
-        nc.sync.dma_start(w2w_raw[:].bitcast(I32), w2_v[:, CH // 2 :])
+        nc.sync.dma_start(w2w_raw[:].bitcast(I32), w2_v[:, EARLY // 2 :])
         for t in range(PACK):
             nc.sync.dma_start(so_sb[t][:], so_v[t])
-        nc.scalar.copy(
-            w2w[:].bitcast(U16).rearrange("p (t m) -> p t m", t=PACK)[:, :, CH // PACK :],
-            w2w_raw[:].bitcast(U16).rearrange("p (m t) -> p t m", t=PACK),
+        nc.gpsimd.tensor_copy(
+            w2w[:].rearrange("p (t m b) -> p t m b", t=PACK, b=2)[:, :, EARLY // PACK :, :],
+            w2w_raw[:].rearrange("p (m t b) -> p t m b", t=PACK, b=2),
         )
 
         word_spans = [(0, CH), (CH, HALF), (HALF, S)]
@@ -157,21 +164,25 @@ def tile_picked_bens8_relu_po_kernel(
             nc.vector.tensor_copy(
                 xw[i][:].bitcast(U32), xw_all[:].bitcast(U32).indirect(offs_sb[:, lo // 16 : hi // 16])
             )
-        for pair in range(2):
-            for h in range(2):
-                for t in (2 * pair, 2 * pair + 1):
-                    pick(scalar_gather, so_picked[h][:, t, :], so_sb[t], h * HALF, (h + 1) * HALF)
+        for t in range(PACK):
+            pick(scalar_gather, so_first[:, t, :], so_sb[t], 0, HALF)
+            if t >= 2:
+                pick(scalar_gather, so_second[1][:, t - 2, :], so_sb[t], HALF, S)
+        for base in (0, CH):
+            for t in range(2):
+                pick(scalar_gather, so_second[0][:, t, base : base + CH], so_sb[t], HALF + base, HALF + base + CH)
 
-        spans = [(0, HALF), (HALF, HALF + CH), (HALF + CH, S)]
+        spans = [(0, HALF), (HALF, S)]
         zbf = [tile(f"zbf_{i}", [P, PACK * (hi - lo)], BF16) for i, (lo, hi) in enumerate(spans)]
         zw = [tile(f"zw_{i}", [P, hi - lo], I32) for i, (lo, hi) in enumerate(spans)]
         zs = [tile(f"zs_{i}", [P, hi - lo], U8) for i, (lo, hi) in enumerate(spans)]
-        y32 = [tile(f"y32_{i}", [P, PACK, hi - lo], F32) for i, (lo, hi) in enumerate(spans)]
+        y_chunk = [tile(f"y_chunk{c}", [P, PACK, CH], F32) for c in range(2)]
+        y_second = tile("y_second", [P, PACK, HALF], F32)
 
         def span_of(c):
-            i = max(c - 1, 0)
-            return i, c * CH - spans[i][0]
-        ybf = [tile(f"ybf_{i}", [P, PACK * (hi - lo)], BF16) for i, (lo, hi) in enumerate(spans)]
+            return divmod(c * CH, HALF)
+
+        ybf = [tile(f"ybf_{c}", [P, PACK * CH], BF16) for c in range(NCH)]
         yw = tile("yw", [P, S], I32)
         ys = tile("ys", [P, S], U8)
         out0_v = out_0.rearrange("(p t) n -> p t n", t=PACK)
@@ -200,60 +211,72 @@ def tile_picked_bens8_relu_po_kernel(
                 MULT,
             )
 
-        def quantize_hidden(h):
-            nc.vector.quantize_mx(out=zw[h][:].bitcast(FP8X4), scales=zs[h][:], in_=zbf[h][:])
+        def quantize_hidden(h, lo, hi):
+            nc.vector.quantize_mx(
+                out=zw[h][:, lo:hi].bitcast(FP8X4), scales=zs[h][:, lo:hi], in_=zbf[h][:, PACK * lo : PACK * hi]
+            )
 
-        def output(i, planes):
-            lo, hi = spans[i]
-            h, base = divmod(lo, HALF)
-            acc = psum.tile([P, len(planes), hi - lo], F32, name=f"acc2_{i}_{planes[0]}")
+        def second_product(name, h, planes, lo, hi):
+            acc = psum.tile([P, len(planes), hi - lo], F32, name=name)
             for n, t in enumerate(planes):
                 nc.tensor.matmul_mx(
                     out=acc[:, n, :],
                     lhsT=w2w[:, 2 * P * t : 2 * P * (t + 1)].bitcast(FP4X4),
                     lhsT_scale=w2s[:, P * t : P * (t + 1)],
-                    rhs=zw[i][:].bitcast(FP8X4),
-                    rhs_scale=zs[i][:],
+                    rhs=zw[h][:, lo:hi].bitcast(FP8X4),
+                    rhs_scale=zs[h][:, lo:hi],
                     start=True,
                     stop=True,
                 )
-            rows = slice(planes[0], planes[-1] + 1)
-            nc.vector.tensor_tensor(y32[i][:, rows, :], acc[:], so_picked[h][:, rows, base : base + hi - lo], MULT)
-            nc.sync.dma_start(out0_v[:, rows, lo:hi], y32[i][:, rows, :])
+            return acc
+
+        def output_chunk(c):
+            lo, hi = c * CH, (c + 1) * CH
+            acc = second_product(f"acc2_{c}", 0, range(PACK), lo, hi)
+            nc.vector.tensor_tensor(y_chunk[c][:], acc[:], so_first[:, :, lo:hi], MULT)
+            nc.sync.dma_start(out0_v[:, :, lo:hi], y_chunk[c][:])
+            nc.gpsimd.tensor_scalar(
+                ybf[c][:].rearrange("p (c t) -> p c t", t=PACK),
+                y_chunk[c][:].rearrange("p t c -> p c t"),
+                1.0,
+                -0.0,
+                MULT,
+                ADD,
+            )
+
+        def output_pair(pair, steps):
+            planes = [2 * pair, 2 * pair + 1]
+            acc = second_product(f"acc2_pair{pair}", 1, planes, 0, HALF)
+            rows = slice(2 * pair, 2 * pair + 2)
+            for lo, hi in steps:
+                nc.vector.tensor_tensor(y_second[:, rows, lo:hi], acc[:, :, lo:hi], so_second[pair][:, :, lo:hi], MULT)
+            nc.sync.dma_start(out0_v[:, rows, HALF:], y_second[:, rows, :])
 
         def round_output(c, copy):
             i, at = span_of(c)
-            weave(copy, ybf[i][:, PACK * at : PACK * (at + CH)], y32[i][:, :, at : at + CH])
+            weave(copy, ybf[c][:], y_second[:, :, at : at + CH])
 
-        def quantize_output(i):
-            lo, hi = spans[i]
-            nc.vector.quantize_mx(out=yw[:, lo:hi].bitcast(FP8X4), scales=ys[:, lo:hi], in_=ybf[i][:])
+        def quantize_output(c):
+            lo, hi = c * CH, (c + 1) * CH
+            nc.vector.quantize_mx(out=yw[:, lo:hi].bitcast(FP8X4), scales=ys[:, lo:hi], in_=ybf[c][:])
 
         for c in range(3):
             hidden(c)
-        quantize_hidden(0)
+        quantize_hidden(0, 0, HALF)
         hidden(3)
-        quantize_hidden(1)
-        output(0, [0, 1])
-        quantize_hidden(2)
-        output(0, [2, 3])
-        for i in (1, 2):
-            output(i, range(PACK))
-        nc.gpsimd.tensor_scalar(
-            ybf[0][:, : PACK * CH].rearrange("p (c t) -> p c t", t=PACK),
-            y32[0][:, :, :CH].rearrange("p t c -> p c t"),
-            1.0,
-            -0.0,
-            MULT,
-            ADD,
-        )
-        for c in (1, 2):
-            round_output(c, nc.scalar.copy)
+        quantize_hidden(1, 0, CH)
+        output_chunk(0)
+        quantize_hidden(1, CH, HALF)
+        output_chunk(1)
+        output_pair(1, [(0, HALF)])
+        output_pair(0, [(0, CH), (CH, HALF)])
+        round_output(2, nc.scalar.copy)
         quantize_output(0)
-        nc.sync.dma_start(out1_v[:, :HALF], yw[:, :HALF])
         round_output(3, nc.vector.tensor_copy)
         quantize_output(1)
+        nc.sync.dma_start(out1_v[:, :HALF], yw[:, :HALF])
         quantize_output(2)
+        quantize_output(3)
         nc.sync.dma_start(out1_v[:, HALF:], yw[:, HALF:])
         for q in range(4):
             eng = nc.scalar if q % 2 else nc.sync

@@ -27,7 +27,7 @@ ROW = 4 * W
 RIN_AT = [4 * ROW, 5 * ROW, 6 * ROW, 9 * ROW]
 SO_AT = [5 * ROW + 256, 7 * ROW - 256, 8 * ROW + ROW // 2, 9 * ROW + ROW // 2]
 W1_VECTOR_SHARE = 80
-EARLY = 192
+EARLY = 32
 
 FLOPS = 2 * 2 * 512 * 512 * 512
 
@@ -69,9 +69,9 @@ def tile_picked_bens8_relu_po_kernel(
         rin_v = rin.rearrange("(p t) u -> t p u", t=PACK)
         so_v = so.rearrange("(p t) u -> t p u", t=PACK)
         w2_v = w2_words[0].bitcast(I32)
-        nc.sync.dma_start(w2w_early[:].bitcast(I32), w2_v[:, : EARLY // 2])
-        nc.sync.dma_start(mem_sb[:], mem)
         nc.sync.dma_start(rin_sb[0][:], rin_v[0])
+        nc.sync.dma_start(mem_sb[:], mem)
+        nc.sync.dma_start(w2w_early[:].bitcast(I32), w2_v[:, : EARLY // 2])
         nc.sync.dma_start(rin_sb[1][:], rin_v[1])
         nc.sync.dma_start(offs_sb[:], offs)
         nc.sync.dma_start(xs_all[0:P:8, :].bitcast(I32), x_scales[0].bitcast(I32))
@@ -137,25 +137,25 @@ def tile_picked_bens8_relu_po_kernel(
 
         def weave_factors(c):
             h, base = divmod(c * CH, HALF)
-            copy = nc.vector.tensor_copy if c < NCH - 1 else nc.scalar.copy
+            copy = nc.scalar.copy if h else nc.vector.tensor_copy
             weave(copy, rin_woven[c][:], rin_picked[h][:, :, base : base + CH])
 
         for c in range(2):
             weave_factors(c)
         nc.vector.tensor_copy(w1_dst[:, :W1_VECTOR_SHARE], w1_src[:, :W1_VECTOR_SHARE])
         nc.scalar.copy(w1_dst[:, W1_VECTOR_SHARE:], w1_src[:, W1_VECTOR_SHARE:])
-        weave_factors(2)
         nc.vector.quantize_mx(out=w1w[:].bitcast(FP8X4), scales=w1s[:], in_=w1_bf[:])
-        weave_factors(NCH - 1)
+        for c in (2, 3):
+            weave_factors(c)
         nc.gpsimd.tensor_copy(
             w2s[:].rearrange("p (t m) -> p t m", t=PACK), w2s_raw[:].rearrange("p (m t) -> p t m", t=PACK)
         )
         nc.sync.dma_start(w2w_raw[:].bitcast(I32), w2_v[:, EARLY // 2 :])
         for t in range(PACK):
             nc.sync.dma_start(so_sb[t][:], so_v[t])
-        nc.gpsimd.tensor_copy(
-            w2w[:].rearrange("p (t m b) -> p t m b", t=PACK, b=2)[:, :, EARLY // PACK :, :],
-            w2w_raw[:].rearrange("p (m t b) -> p t m b", t=PACK, b=2),
+        nc.scalar.copy(
+            w2w[:].bitcast(U16).rearrange("p (t m) -> p t m", t=PACK)[:, :, EARLY // PACK :],
+            w2w_raw[:].bitcast(U16).rearrange("p (m t) -> p t m", t=PACK),
         )
 
         word_spans = [(0, CH), (CH, HALF), (HALF, S)]

@@ -12,7 +12,6 @@ FP8X4 = mybir.dt.float8_e4m3fn_x4
 FP4X4 = mybir.dt.float4_e2m1fn_x4
 COPY = mybir.ActivationFunctionType.Copy
 MULT = mybir.AluOpType.mult
-ADD = mybir.AluOpType.add
 MAX = mybir.AluOpType.max
 
 P = 128
@@ -235,14 +234,6 @@ def tile_picked_bens8_relu_po_kernel(
             acc = second_product(f"acc2_{c}", 0, range(PACK), lo, hi)
             nc.vector.tensor_tensor(y_chunk[c][:], acc[:], so_first[:, :, lo:hi], MULT)
             nc.sync.dma_start(out0_v[:, :, lo:hi], y_chunk[c][:])
-            nc.gpsimd.tensor_scalar(
-                ybf[c][:].rearrange("p (c t) -> p c t", t=PACK),
-                y_chunk[c][:].rearrange("p t c -> p c t"),
-                1.0,
-                -0.0,
-                MULT,
-                ADD,
-            )
 
         def output_pair(pair, steps):
             planes = [2 * pair, 2 * pair + 1]
@@ -253,8 +244,8 @@ def tile_picked_bens8_relu_po_kernel(
             nc.sync.dma_start(out0_v[:, rows, HALF:], y_second[:, rows, :])
 
         def round_output(c, copy):
-            i, at = span_of(c)
-            weave(copy, ybf[c][:], y_second[:, :, at : at + CH])
+            h, at = span_of(c)
+            weave(copy, ybf[c][:], y_second[:, :, at : at + CH] if h else y_chunk[c][:])
 
         def quantize_output(c):
             lo, hi = c * CH, (c + 1) * CH
@@ -268,9 +259,11 @@ def tile_picked_bens8_relu_po_kernel(
         output_chunk(0)
         quantize_hidden(1, CH, HALF)
         output_chunk(1)
+        round_output(0, nc.vector.tensor_copy)
         output_pair(1, [(0, HALF)])
         output_pair(0, [(0, CH), (CH, HALF)])
-        round_output(2, nc.scalar.copy)
+        for c in (1, 2):
+            round_output(c, nc.scalar.copy)
         quantize_output(0)
         round_output(3, nc.vector.tensor_copy)
         quantize_output(1)

@@ -12,6 +12,7 @@ FP8X4 = mybir.dt.float8_e4m3fn_x4
 FP4X4 = mybir.dt.float4_e2m1fn_x4
 COPY = mybir.ActivationFunctionType.Copy
 MULT = mybir.AluOpType.mult
+ADD = mybir.AluOpType.add
 MAX = mybir.AluOpType.max
 
 P = 128
@@ -257,9 +258,16 @@ def tile_picked_bens8_relu_po_kernel(
         hidden(3)
         quantize_hidden(1, 0, CH)
         output_chunk(0)
+        nc.gpsimd.tensor_scalar(
+            ybf[0][:].rearrange("p (c t) -> p c t", t=PACK),
+            y_chunk[0][:].rearrange("p t c -> p c t"),
+            1.0,
+            -0.0,
+            MULT,
+            ADD,
+        )
         quantize_hidden(1, CH, HALF)
         output_chunk(1)
-        round_output(0, nc.vector.tensor_copy)
         output_pair(1, [(0, HALF)])
         output_pair(0, [(0, CH), (CH, HALF)])
         for c in (1, 2):

@@ -168,9 +168,8 @@ def tile_picked_bens8_relu_po_kernel(
             pick(scalar_gather, so_first[:, t, :], so_sb[t], 0, HALF)
             if t >= 2:
                 pick(scalar_gather, so_second[1][:, t - 2, :], so_sb[t], HALF, S)
-        for base in (0, CH):
-            for t in range(2):
-                pick(scalar_gather, so_second[0][:, t, base : base + CH], so_sb[t], HALF + base, HALF + base + CH)
+        for t in range(2):
+            pick(scalar_gather, so_second[0][:, t, :], so_sb[t], HALF, S)
 
         spans = [(0, HALF), (HALF, S)]
         zbf = [tile(f"zbf_{i}", [P, PACK * (hi - lo)], BF16) for i, (lo, hi) in enumerate(spans)]
@@ -240,8 +239,13 @@ def tile_picked_bens8_relu_po_kernel(
             planes = [2 * pair, 2 * pair + 1]
             acc = second_product(f"acc2_pair{pair}", 1, planes, 0, HALF)
             rows = slice(2 * pair, 2 * pair + 2)
-            for lo, hi in steps:
-                nc.vector.tensor_tensor(y_second[:, rows, lo:hi], acc[:, :, lo:hi], so_second[pair][:, :, lo:hi], MULT)
+            for first, last, lo, hi in steps:
+                nc.vector.tensor_tensor(
+                    y_second[:, 2 * pair + first : 2 * pair + last, lo:hi],
+                    acc[:, first:last, lo:hi],
+                    so_second[pair][:, first:last, lo:hi],
+                    MULT,
+                )
             nc.sync.dma_start(out0_v[:, rows, HALF:], y_second[:, rows, :])
 
         def round_output(c, copy):
@@ -252,11 +256,14 @@ def tile_picked_bens8_relu_po_kernel(
             lo, hi = c * CH, (c + 1) * CH
             nc.vector.quantize_mx(out=yw[:, lo:hi].bitcast(FP8X4), scales=ys[:, lo:hi], in_=ybf[c][:])
 
-        for c in range(3):
-            hidden(c)
-        quantize_hidden(0, 0, HALF)
+        hidden(0)
+        hidden(1)
+        quantize_hidden(0, 0, CH)
+        hidden(2)
+        quantize_hidden(0, CH, HALF)
         hidden(3)
         quantize_hidden(1, 0, CH)
+        quantize_hidden(1, CH, HALF)
         output_chunk(0)
         nc.gpsimd.tensor_scalar(
             ybf[0][:].rearrange("p (c t) -> p c t", t=PACK),
@@ -266,18 +273,17 @@ def tile_picked_bens8_relu_po_kernel(
             MULT,
             ADD,
         )
-        quantize_hidden(1, CH, HALF)
         output_chunk(1)
-        output_pair(1, [(0, HALF)])
-        output_pair(0, [(0, CH), (CH, HALF)])
+        output_pair(1, [(0, 2, 0, HALF)])
+        output_pair(0, [(0, 1, 0, HALF), (1, 2, 0, CH), (1, 2, CH, HALF)])
         for c in (1, 2):
             round_output(c, nc.scalar.copy)
         quantize_output(0)
         round_output(3, nc.vector.tensor_copy)
         quantize_output(1)
         nc.sync.dma_start(out1_v[:, :HALF], yw[:, :HALF])
-        quantize_output(2)
         quantize_output(3)
+        quantize_output(2)
         nc.sync.dma_start(out1_v[:, HALF:], yw[:, HALF:])
         for q in range(4):
             eng = nc.scalar if q % 2 else nc.sync

@@ -24,6 +24,7 @@ HALF = 256
 CH = 128
 NCH = S // CH
 ROW = 4 * W
+ALIGN = 256
 RIN_AT = [4 * ROW, 5 * ROW, 6 * ROW, 9 * ROW]
 SO_AT = [5 * ROW + 256, 7 * ROW - 256, 8 * ROW + ROW // 2, 9 * ROW + ROW // 2]
 W1_VECTOR_SHARE = 80
@@ -42,7 +43,7 @@ def tile_picked_bens8_relu_po_kernel(
         psum = ctx.enter_context(tc.psum_pool(name="psum", bufs=1))
 
         def tile(name, shape, dtype):
-            return keep.tile(shape, dtype, name=name, align_bytes=64)
+            return keep.tile(shape, dtype, name=name, align_bytes=ALIGN)
 
         offs_sb = tile("offs_sb", [P, S // 16], U16)
         mem_sb = tile("mem_sb", [P, S // 16], U16)
@@ -50,17 +51,17 @@ def tile_picked_bens8_relu_po_kernel(
         xs_all = tile("xs_all", [P, T], U8)
         xs_picked = tile("xs_picked", [P, S], U8)
         xs = tile("xs", [P, S], U8)
-        w1_raw = reuse.tile([P, PACK, W], F32, name="w1_raw", offset=0, align_bytes=64)
-        w2w_raw = reuse.tile([P, 2 * (W - EARLY)], U8, name="w2w_raw", offset=RIN_AT[2] + 256, align_bytes=64)
+        w1_raw = reuse.tile([P, PACK, W], F32, name="w1_raw", offset=0, align_bytes=ALIGN)
+        w2w_raw = reuse.tile([P, 2 * (W - EARLY)], U8, name="w2w_raw", offset=RIN_AT[2] + 256, align_bytes=ALIGN)
         w2s_raw = tile("w2s_raw", [P, W], U8)
         w2w_early = tile("w2w_early", [P, 2 * EARLY], U8)
         w2w = tile("w2w", [P, 2 * W], U8)
         w2s = tile("w2s", [P, W], U8)
         rin_sb = [
-            reuse.tile([P, W], F32, name=f"rin{t}", offset=RIN_AT[t], align_bytes=64) for t in range(PACK)
+            reuse.tile([P, W], F32, name=f"rin{t}", offset=RIN_AT[t], align_bytes=ALIGN) for t in range(PACK)
         ]
         so_sb = [
-            reuse.tile([P, W], F32, name=f"so{t}", offset=SO_AT[t], align_bytes=64) for t in range(PACK)
+            reuse.tile([P, W], F32, name=f"so{t}", offset=SO_AT[t], align_bytes=ALIGN) for t in range(PACK)
         ]
 
         nc.vector.memset(xs_all[:].bitcast(I32), 0)
@@ -118,11 +119,11 @@ def tile_picked_bens8_relu_po_kernel(
         rin_picked = [tile(f"rin_picked{h}", [P, PACK, HALF], F32) for h in range(2)]
         rin_woven = [tile(f"rin_woven{c}", [P, PACK * CH], F32) for c in range(2)]
         rin_woven.extend(
-            reuse.tile([P, PACK * CH], F32, name=f"rin_woven{c}", offset=c * ROW, align_bytes=64) for c in (2, 3)
+            reuse.tile([P, PACK * CH], F32, name=f"rin_woven{c}", offset=c * ROW, align_bytes=ALIGN) for c in (2, 3)
         )
         so_first = tile("so_first", [P, PACK, HALF], F32)
         so_second = [
-            reuse.tile([P, 2, HALF], F32, name="so_second0", offset=SO_AT[3], align_bytes=64),
+            reuse.tile([P, 2, HALF], F32, name="so_second0", offset=SO_AT[3], align_bytes=ALIGN),
             tile("so_second1", [P, 2, HALF], F32),
         ]
 

from contextlib import ExitStack

import concourse.mybir as mybir

F32 = mybir.dt.float32
BF16 = mybir.dt.bfloat16
I32 = mybir.dt.int32
U32 = mybir.dt.uint32
U16 = mybir.dt.uint16
U8 = mybir.dt.uint8
FP8X4 = mybir.dt.float8_e4m3fn_x4
FP4X4 = mybir.dt.float4_e2m1fn_x4
COPY = mybir.ActivationFunctionType.Copy
MULT = mybir.AluOpType.mult
ADD = mybir.AluOpType.add
MAX = mybir.AluOpType.max

P = 128
PACK = 4
T = 2048
S = 512
W = 512
HALF = 256
CH = 128
NCH = S // CH
ROW = 4 * W
ALIGN = 256
RIN_AT = [4 * ROW, 5 * ROW, 6 * ROW, 9 * ROW]
SO_AT = [5 * ROW + 256, 7 * ROW - 256, 8 * ROW + ROW // 2, 9 * ROW + ROW // 2]
W1_VECTOR_SHARE = 80
EARLY = 32

FLOPS = 2 * 2 * 512 * 512 * 512


def tile_picked_bens8_relu_po_kernel(
    tc, x_words, x_scales, w1, rin, w2_words, w2_scales, so, offs, mem, out_0, out_1, out_2
):
    nc = tc.nc
    with ExitStack() as ctx:
        keep = ctx.enter_context(tc.tile_pool(name="keep", bufs=1))
        reuse = ctx.enter_context(tc.tile_pool(name="reuse", bufs=1))
        psum = ctx.enter_context(tc.psum_pool(name="psum", bufs=1))

        def tile(name, shape, dtype):
            return keep.tile(shape, dtype, name=name, align_bytes=ALIGN)

        offs_sb = tile("offs_sb", [P, S // 16], U16)
        mem_sb = tile("mem_sb", [P, S // 16], U16)
        xw_all = tile("xw_all", [P, T], I32)
        xs_all = tile("xs_all", [P, T], U8)
        xs_picked = tile("xs_picked", [P, S], U8)
        xs = tile("xs", [P, S], U8)
        w1_raw = reuse.tile([P, PACK, W], F32, name="w1_raw", offset=0, align_bytes=ALIGN)
        w2w_raw = reuse.tile([P, 2 * (W - EARLY)], U8, name="w2w_raw", offset=RIN_AT[2] + 256, align_bytes=ALIGN)
        w2s_raw = tile("w2s_raw", [P, W], U8)
        w2w_early = tile("w2w_early", [P, 2 * EARLY], U8)
        w2w = tile("w2w", [P, 2 * W], U8)
        w2s = tile("w2s", [P, W], U8)
        rin_sb = [
            reuse.tile([P, W], F32, name=f"rin{t}", offset=RIN_AT[t], align_bytes=ALIGN) for t in range(PACK)
        ]
        so_sb = [
            reuse.tile([P, W], F32, name=f"so{t}", offset=SO_AT[t], align_bytes=ALIGN) for t in range(PACK)
        ]

        nc.vector.memset(xs_all[:].bitcast(I32), 0)
        nc.gpsimd.memset(w2s_raw[:].bitcast(I32), 0)

        rin_v = rin.rearrange("(p t) u -> t p u", t=PACK)
        so_v = so.rearrange("(p t) u -> t p u", t=PACK)
        w2_v = w2_words[0].bitcast(I32)
        nc.sync.dma_start(rin_sb[0][:], rin_v[0])
        nc.sync.dma_start(mem_sb[:], mem)
        nc.sync.dma_start(w2w_early[:].bitcast(I32), w2_v[:, : EARLY // 2])
        nc.sync.dma_start(rin_sb[1][:], rin_v[1])
        nc.sync.dma_start(offs_sb[:], offs)
        nc.sync.dma_start(xs_all[0:P:8, :].bitcast(I32), x_scales[0].bitcast(I32))
        for t in range(2, PACK):
            nc.sync.dma_start(rin_sb[t][:], rin_v[t])
        nc.sync.dma_start(w1_raw[:], w1.rearrange("(p j) c -> p j c", j=PACK))
        nc.sync.dma_start(xw_all[:], x_words[0].rearrange("p c r -> p (c r)").bitcast(I32))
        for q in range(4):
            nc.gpsimd.dma_start(
                w2s_raw[32 * q : 32 * q + 4, :].bitcast(I32), w2_scales[0, 4 * q : 4 * q + 4, :].bitcast(I32)
            )

        nc.vector.tensor_copy(xs_picked[:], xs_all[:].indirect(offs_sb[:]))
        nc.vector.tensor_copy(xs[:].bitcast(I32), xs_picked[:].bitcast(I32))
        for r in range(1, 4):
            nc.sync.dma_start(xs[r:P:32, :].bitcast(I32), xs_picked[8 * r : P : 32, :].bitcast(I32))

        nc.scalar.copy(
            w2w[:].bitcast(U16).rearrange("p (t m) -> p t m", t=PACK)[:, :, : EARLY // PACK],
            w2w_early[:].bitcast(U16).rearrange("p (m t) -> p t m", t=PACK),
        )

        w1_bf = tile("w1_bf", [P, PACK * W], BF16)
        w1_dst = w1_bf[:].rearrange("p (t m j) -> p m j t", t=PACK, j=PACK)
        w1_src = w1_raw[:].rearrange("p j (m t) -> p m j t", t=PACK)
        w1w = tile("w1w", [P, W], I32)
        w1s = tile("w1s", [P, W], U8)

        def scalar_gather(dst, window):
            nc.scalar.activation(dst, window, COPY)

        def pick(gather, dst, table, lo, hi):
            gather(dst, table[:].indirect(mem_sb[:, lo // 16 : hi // 16]))

        def woven(ap):
            return ap.rearrange("p (c i t) -> p c t i", i=4, t=PACK)

        def by_planes(ap):
            return ap.rearrange("p t (c i) -> p c t i", i=4)

        def weave(copy, dst, src):
            copy(woven(dst), by_planes(src))

        rin_picked = [tile(f"rin_picked{h}", [P, PACK, HALF], F32) for h in range(2)]
        rin_woven = [tile(f"rin_woven{c}", [P, PACK * CH], F32) for c in range(2)]
        rin_woven.extend(
            reuse.tile([P, PACK * CH], F32, name=f"rin_woven{c}", offset=c * ROW, align_bytes=ALIGN) for c in (2, 3)
        )
        so_first = tile("so_first", [P, PACK, HALF], F32)
        so_second = [
            reuse.tile([P, 2, HALF], F32, name="so_second0", offset=SO_AT[3], align_bytes=ALIGN),
            tile("so_second1", [P, 2, HALF], F32),
        ]

        for h in range(2):
            pick(nc.vector.tensor_copy, rin_picked[h][:, 0, :], rin_sb[0], h * HALF, (h + 1) * HALF)
        for h in range(2):
            pick(scalar_gather, rin_picked[h][:, 1, :], rin_sb[1], h * HALF, (h + 1) * HALF)
        for h in range(2):
            pick(scalar_gather, rin_picked[h][:, 2, :], rin_sb[2], h * HALF, (h + 1) * HALF)
        pick(nc.vector.tensor_copy, rin_picked[0][:, 3, :], rin_sb[3], 0, HALF)
        pick(scalar_gather, rin_picked[1][:, 3, :], rin_sb[3], HALF, S)

        def weave_factors(c):
            h, base = divmod(c * CH, HALF)
            copy = nc.scalar.copy if h else nc.vector.tensor_copy
            weave(copy, rin_woven[c][:], rin_picked[h][:, :, base : base + CH])

        for c in range(2):
            weave_factors(c)
        nc.vector.tensor_copy(w1_dst[:, :W1_VECTOR_SHARE], w1_src[:, :W1_VECTOR_SHARE])
        nc.scalar.copy(w1_dst[:, W1_VECTOR_SHARE:], w1_src[:, W1_VECTOR_SHARE:])
        nc.vector.quantize_mx(out=w1w[:].bitcast(FP8X4), scales=w1s[:], in_=w1_bf[:])
        for c in (2, 3):
            weave_factors(c)
        nc.gpsimd.tensor_copy(
            w2s[:].rearrange("p (t m) -> p t m", t=PACK), w2s_raw[:].rearrange("p (m t) -> p t m", t=PACK)
        )
        nc.sync.dma_start(w2w_raw[:].bitcast(I32), w2_v[:, EARLY // 2 :])
        for t in range(PACK):
            nc.sync.dma_start(so_sb[t][:], so_v[t])
        nc.scalar.copy(
            w2w[:].bitcast(U16).rearrange("p (t m) -> p t m", t=PACK)[:, :, EARLY // PACK :],
            w2w_raw[:].bitcast(U16).rearrange("p (m t) -> p t m", t=PACK),
        )

        word_spans = [(0, CH), (CH, HALF), (HALF, S)]
        xw = [tile(f"xw{i}", [P, hi - lo], I32) for i, (lo, hi) in enumerate(word_spans)]
        for i, (lo, hi) in enumerate(word_spans):
            nc.vector.tensor_copy(
                xw[i][:].bitcast(U32), xw_all[:].bitcast(U32).indirect(offs_sb[:, lo // 16 : hi // 16])
            )
        for t in range(PACK):
            pick(scalar_gather, so_first[:, t, :], so_sb[t], 0, HALF)
            if t >= 2:
                pick(scalar_gather, so_second[1][:, t - 2, :], so_sb[t], HALF, S)
        for t in range(2):
            pick(scalar_gather, so_second[0][:, t, :], so_sb[t], HALF, S)

        spans = [(0, HALF), (HALF, S)]
        zbf = [tile(f"zbf_{i}", [P, PACK * (hi - lo)], BF16) for i, (lo, hi) in enumerate(spans)]
        zw = [tile(f"zw_{i}", [P, hi - lo], I32) for i, (lo, hi) in enumerate(spans)]
        zs = [tile(f"zs_{i}", [P, hi - lo], U8) for i, (lo, hi) in enumerate(spans)]
        y_chunk = [tile(f"y_chunk{c}", [P, PACK, CH], F32) for c in range(2)]
        y_second = tile("y_second", [P, PACK, HALF], F32)

        def span_of(c):
            return divmod(c * CH, HALF)

        ybf = [tile(f"ybf_{c}", [P, PACK * CH], BF16) for c in range(NCH)]
        yw = tile("yw", [P, S], I32)
        ys = tile("ys", [P, S], U8)
        out0_v = out_0.rearrange("(p t) n -> p t n", t=PACK)
        out1_v = out_1[0].rearrange("p c r -> p (c r)").bitcast(I32)

        def hidden(c):
            h, base = span_of(c)
            words = xw[min(c, 2)][:, (c == 3) * CH : (c == 3) * CH + CH]
            acc = psum.tile([P, PACK, CH], F32, name=f"acc1_{c}")
            for t in range(PACK):
                nc.tensor.matmul_mx(
                    out=acc[:, t, :],
                    lhsT=w1w[:, P * t : P * (t + 1)].bitcast(FP8X4),
                    lhsT_scale=w1s[:, P * t : P * (t + 1)],
                    rhs=words.bitcast(FP8X4),
                    rhs_scale=xs[:, c * CH : (c + 1) * CH],
                    start=True,
                    stop=True,
                )
            nc.vector.scalar_tensor_tensor(
                zbf[h][:, PACK * base : PACK * (base + CH)].rearrange("p (c t) -> p c t", t=PACK),
                acc[:].rearrange("p t c -> p c t"),
                0.0,
                rin_woven[c][:].rearrange("p (c t) -> p c t", t=PACK),
                MAX,
                MULT,
            )

        def quantize_hidden(h, lo, hi):
            nc.vector.quantize_mx(
                out=zw[h][:, lo:hi].bitcast(FP8X4), scales=zs[h][:, lo:hi], in_=zbf[h][:, PACK * lo : PACK * hi]
            )

        def second_product(name, h, planes, lo, hi):
            acc = psum.tile([P, len(planes), hi - lo], F32, name=name)
            for n, t in enumerate(planes):
                nc.tensor.matmul_mx(
                    out=acc[:, n, :],
                    lhsT=w2w[:, 2 * P * t : 2 * P * (t + 1)].bitcast(FP4X4),
                    lhsT_scale=w2s[:, P * t : P * (t + 1)],
                    rhs=zw[h][:, lo:hi].bitcast(FP8X4),
                    rhs_scale=zs[h][:, lo:hi],
                    start=True,
                    stop=True,
                )
            return acc

        def output_chunk(c):
            lo, hi = c * CH, (c + 1) * CH
            acc = second_product(f"acc2_{c}", 0, range(PACK), lo, hi)
            nc.vector.tensor_tensor(y_chunk[c][:], acc[:], so_first[:, :, lo:hi], MULT)
            nc.sync.dma_start(out0_v[:, :, lo:hi], y_chunk[c][:])

        def output_pair(pair, steps):
            planes = [2 * pair, 2 * pair + 1]
            acc = second_product(f"acc2_pair{pair}", 1, planes, 0, HALF)
            rows = slice(2 * pair, 2 * pair + 2)
            for first, last, lo, hi in steps:
                nc.vector.tensor_tensor(
                    y_second[:, 2 * pair + first : 2 * pair + last, lo:hi],
                    acc[:, first:last, lo:hi],
                    so_second[pair][:, first:last, lo:hi],
                    MULT,
                )
            nc.sync.dma_start(out0_v[:, rows, HALF:], y_second[:, rows, :])

        def round_output(c, copy):
            h, at = span_of(c)
            weave(copy, ybf[c][:], y_second[:, :, at : at + CH] if h else y_chunk[c][:])

        def quantize_output(c):
            lo, hi = c * CH, (c + 1) * CH
            nc.vector.quantize_mx(out=yw[:, lo:hi].bitcast(FP8X4), scales=ys[:, lo:hi], in_=ybf[c][:])

        hidden(0)
        hidden(1)
        quantize_hidden(0, 0, CH)
        hidden(2)
        quantize_hidden(0, CH, HALF)
        hidden(3)
        quantize_hidden(1, 0, CH)
        quantize_hidden(1, CH, HALF)
        output_chunk(0)
        nc.gpsimd.tensor_scalar(
            ybf[0][:].rearrange("p (c t) -> p c t", t=PACK),
            y_chunk[0][:].rearrange("p t c -> p c t"),
            1.0,
            -0.0,
            MULT,
            ADD,
        )
        output_chunk(1)
        output_pair(1, [(0, 2, 0, HALF)])
        output_pair(0, [(0, 1, 0, HALF), (1, 2, 0, CH), (1, 2, CH, HALF)])
        for c in (1, 2):
            round_output(c, nc.scalar.copy)
        quantize_output(0)
        round_output(3, nc.vector.tensor_copy)
        quantize_output(1)
        nc.sync.dma_start(out1_v[:, :HALF], yw[:, :HALF])
        quantize_output(3)
        quantize_output(2)
        nc.sync.dma_start(out1_v[:, HALF:], yw[:, HALF:])
        for q in range(4):
            eng = nc.scalar if q % 2 else nc.sync
            eng.dma_start(out_2[0, 4 * q : 4 * q + 4, :].bitcast(I32), ys[32 * q : 32 * q + 4, :].bitcast(I32))
